import numpy as np, ml_dtypes
CORES = [48,51,52,55]
N = 4
BF = ml_dtypes.bfloat16
H, W, V, K, F, S, R, CAP = 3904, 4096, 1024, 256, 4, 3, 3, 64
def start(q, ans):
    s = np.add.reduce(np.arange(1, 17)[:, None] * q, axis=-2) + ans
    return F * np.arange(K) + (s & (F - 1))
def parts(rng):
    return (rng.integers(0, 256, (N, 8, 16, H)), rng.integers(0, 256, (N, 8, 16, K)), rng.integers(0, H, (N, 8, 16, V)),
            np.ascontiguousarray(np.argsort(rng.random((N, 8, V)), axis=-1)), rng.integers(800, 961, (N, 8)))
def pack(x, q, p, mo, th):
    return {"x": np.ascontiguousarray(x).reshape(N, 128, H).astype(np.float32).astype(BF), "qs": np.ascontiguousarray(q).reshape(N, 128, K).astype(np.float32).astype(BF),
            "towns": np.ascontiguousarray(p).reshape(N, 128, V).astype(np.int32), "mo": np.ascontiguousarray(mo).astype(np.int32),
            "th": np.repeat(th, 16, axis=1).reshape(N, 128, 1).astype(np.int32)}
def mothers(rng, src, dst):
    m = np.zeros(V, np.int64); i = np.arange(V)
    m[src] = dst; m[np.setdiff1d(i, src)] = rng.permutation(np.setdiff1d(i, dst))
    return m
def setup_inputs(rng):
    return pack(*parts(rng))
def setup_inputs_room(rng):
    x, q, p, mo, th = parts(rng)
    x = rng.integers(0, 112, x.shape); th = rng.integers(1, 17, (N, 8))
    for a in range(N):
        for g in range(8):
            n = int(rng.choice(np.array([0, 1, CAP - 1, CAP, CAP + 1, K])))
            if a == 0: n = (CAP, CAP + 1, CAP - 1, 0, 1, K, CAP, K - 1)[g]
            hard = np.zeros(K, bool); hard[rng.permutation(K)[:n]] = True
            rec = rng.integers(0, H - K, K)
            w = np.where(hard, rng.integers(128, 256, (16, K)), x[a, g][:, rec]); w[0, hard] = 128 + 16 * a
            q[a, g] = w; u = start(w, 0)
            e = np.flatnonzero(~hard); p[a, g][rng.integers(0, 8, len(e)), u[e]] = rec[e]
            v = u
            for s in range(S): v = mo[a, g][v]
            b = np.flatnonzero(hard); b = b[rng.random(len(b)) < 0.5]; o = (a + 1) % N
            x[o, g][:, H - K + b] = w[:, b]; p[o, g][rng.integers(8, 16, len(b)), v[b]] = H - K + b
    return pack(x, q, p, mo, th)
def setup_inputs_ties(rng):
    x, q, p, mo, th = parts(rng); o = rng.permutation(8); i, e = o[:4], o[4:]
    x[:, i] = 64 * rng.integers(0, 4, (N, 4, 16, H)); q[:, i] = 64 * rng.integers(0, 4, (N, 4, 16, K))
    y = p[:, i]; y[:, :, 8:, 1::3] = y[:, :, :8, 1::3]; p[:, i] = y
    th[:, i] = rng.choice(np.array([768, 769, 832, 833, 896]), (N, 4))
    k = rng.integers(0, 3, (N, 4, 1, H)); y = np.where(k == 0, 0, np.where(k == 1, 255, x[:, e])); y[..., 0] = 255; x[:, e] = y
    k = rng.integers(0, 3, (N, 4, 1, K)); q[:, e] = np.where(k == 0, 0, np.where(k == 1, 255, q[:, e]))
    y = p[:, e]; y[..., ::5] = 0; p[:, e] = y
    th[:, e] = np.concatenate([rng.permutation(np.array([0, 1, 800, 900, 2000, 4080, 4081, 4096])) for a in range((N + 1) // 2)])[:4 * N].reshape(N, 4)
    return pack(x, q, p, mo, th)
def setup_inputs_alike(rng):
    x, q, p, mo, th = parts(rng)
    pool = rng.integers(0, H, (N, 8, 40)); pool[..., 0] = 0; pool[..., 1] = H - 1
    p = np.take_along_axis(pool, rng.integers(0, 40, (N, 8, 16 * V)), 2).reshape(N, 8, 16, V)
    q[:, :, :, 1::2] = q[:, :, :, 0::2]
    o = rng.permutation(8); i = np.arange(V)
    mo[:, o[0]] = i; mo[:, o[1]] = (i + 1) % V; mo[:, o[2]] = V - 1 - i
    return pack(x, q, p, mo, rng.integers(850, 1001, (N, 8)))
def setup_inputs_crowd(rng):
    x, q, p, mo, th = parts(rng)
    x = rng.integers(0, 96, x.shape); p = rng.integers(0, H - 2 * K, p.shape); th = rng.integers(400, 513, (N, 8))
    for a in range(0, N, 2):
        o = a + 1
        for g in range(8):
            hard = np.zeros(K, bool); hard[rng.permutation(K)[:CAP]] = True
            rec = rng.integers(0, H - 2 * K, K)
            w = x[a, g][:, rec] + rng.integers(0, 8, (16, K)); w[:, hard] = rng.integers(240, 256, (16, CAP))
            q[a, g] = w; u = start(w, 0)
            e = np.flatnonzero(~hard); p[a, g][rng.integers(0, 16, len(e)), u[e]] = rec[e]
            b = np.flatnonzero(hard); c = K * int(rng.integers(0, F))
            free = rng.permutation(np.setdiff1d(np.arange(c, c + K), u[b]))
            way = np.concatenate([u[b], free[:S * CAP]]).reshape(S + 1, CAP)
            mo[a, g] = mothers(rng, way[:-1].reshape(-1), way[1:].reshape(-1))
            x[o, g][:, H - K:H - K + CAP] = 8 * rng.integers(30, 32, (16, CAP))
            p[o, g][rng.integers(8, 16, CAP), way[S]] = H - K + np.arange(CAP)
            x[o, g][:, H - 2 * K:H - K] = rng.integers(136, 200, (16, K))
            if g % 2 == 0: rec = np.full(K, H - 2 * K)
            else:
                rec = H - 2 * K + rng.permutation(K); rec[K - 1] = rec[0]
            w = x[o, g][:, rec] + rng.integers(-8, 9, (16, K))
            q[o, g] = w; u = start(w, 0)
            free = rng.permutation(np.setdiff1d(np.arange(V), u))
            if g // 2 % 2 == 0: free = free[np.argsort(free // K != int(rng.integers(0, F)), kind="stable")]
            v = rng.permutation(free[:K]); mo[o, g] = mothers(rng, u, v)
            p[o, g][rng.integers(0, 8, K), v] = rec
    z = rng.integers(0, H, (N, 8, 1, 1))
    return pack(np.take_along_axis(x, (np.arange(H) - z) % H, 3), q, (p + z) % H, mo, th)
def setup_inputs_spread(rng):
    x, q, p, mo, th = parts(rng)
    x = np.minimum((np.exp2(8.2 * rng.random((N, 8, 1, H))) * rng.random((N, 8, 16, H))).astype(np.int64), 255)
    q = np.minimum((np.exp2(8.2 * rng.random((N, 8, 1, K))) * rng.random((N, 8, 16, K))).astype(np.int64), 255)
    return pack(x, q, p, mo, np.exp2(5 + 6 * rng.random((N, 8))).astype(np.int64))
def check_inputs(d):
    bad = []
    for k in ("x", "qs"):
        v = np.asarray(d[k]).astype(np.float64)
        if not np.all((v >= 0) & (v <= 255) & (v == np.floor(v))): bad.append("whole numbers from 0 to 255 in " + k)
    if np.min(d["towns"]) < 0 or np.max(d["towns"]) > H - 1: bad.append("range of towns")
    m = np.sort(np.asarray(d["mo"]), axis=-1)
    if not np.array_equal(m, np.broadcast_to(np.arange(V), m.shape)): bad.append("the mothers of a group are all different")
    t = np.asarray(d["th"]).reshape(-1, 16)
    if np.min(t) < 0 or np.max(t) > 4096: bad.append("range of th")
    if not np.all(t == t[:, :1]): bad.append("one threshold a group")
    return bad
def tries(rec, lists, u, q, th):
    li = np.take_along_axis(lists, u[:, None, :], 2)
    col = np.take_along_axis(rec, li.reshape(8, 1, 16 * K), 2).reshape(8, 16, 16, K)
    dist = np.add.reduce(np.abs(col - q[:, :, None, :]), axis=1)
    best = np.argmin(dist, axis=1); worst = np.argmax(dist, axis=1)
    num = np.take_along_axis(li, best[:, None, :], 1)[:, 0]
    return np.min(dist, axis=1) < th[:, None], num, worst, li
def reference(x, qs, towns, mo, th):
    X = np.zeros((N, 8, 16, W), np.int32); X[..., :H] = x.astype(np.float32).astype(np.int32).reshape(N, 8, 16, H)
    q = qs.astype(np.float32).astype(np.int32).reshape(N, 8, 16, K)
    P = towns.astype(np.int64).reshape(N, 8, 16, V); M = mo.astype(np.int64); T = th.reshape(N, 8, 16)[:, :, 0].astype(np.int64)
    ans = np.zeros((N, K), np.int64)
    for t in range(R):
        X1, P1, M1, q1, ans1 = X.copy(), P.copy(), M.copy(), q.copy(), ans.copy()
        for a in range(N):
            u = start(q[a].astype(np.int64), ans[a][None, :]); home = np.zeros((8, K), bool); num = np.zeros((8, K), np.int64); path = []
            for s in range(S):
                ok, nm, worst, li = tries(X[a], P[a], u, q[a], T[a])
                hit = ok & ~home; fail = ~ok & ~home
                num = np.where(hit, nm, num); path.append((u, fail, worst, li)); home = home | hit
                u = np.where(fail, np.take_along_axis(M[a], u, 1), u)
            slot = np.add.accumulate((~home).astype(np.int64), axis=1) - 1; place = H + CAP * t + slot
            o = (a + 1 + t) % N
            ok, nm, worst, li = tries(X[o], P[o], u, q[a], T[o])
            came = ok & ~home & (slot < CAP); got = home | came
            old = np.where(home[:, None, :], np.take_along_axis(X[a], num[:, None, :], 2), np.take_along_axis(X[o], nm[:, None, :], 2))
            num = np.where(came, place, num)
            for g in range(8):
                for u_, fail, worst, li in path[::-1]:
                    j = np.flatnonzero(fail[g] & got[g]); new = li[g][:, j]; new[worst[g, j], np.arange(len(j))] = num[g, j]
                    P1[a, g][:, u_[g, j]] = new
                u0, f0 = path[0][0][g], path[0][1][g]
                k = np.flatnonzero(f0[0::2] & f0[1::2]); v, w = u0[2 * k], u0[2 * k + 1]
                M1[a, g, v] = M[a, g, w]; M1[a, g, w] = M[a, g, v]
                j = np.flatnonzero(home[g]); r, i = np.unique(num[g, j], return_index=True); j = j[i]
                X1[a, g][:, r] = (X[a, g][:, r] + q[a, g][:, j]) >> 1
                j = np.flatnonzero(came[g]); X1[a, g][:, place[g, j]] = old[g][:, j]
            q1[a] = np.where(got[:, None, :], (q[a] + old) & 255, q[a])
            ans1[a] = np.add.reduce(got.astype(np.int64), axis=0)
        X, P, M, q, ans = X1, P1, M1, q1, ans1
    return {"yx": X.reshape(N, 128, W).astype(np.float32).astype(BF), "yp": P.reshape(N, 128, V).astype(np.float32), "ym": M.astype(np.float32)}

@@ -1,0 +1,584 @@
+from concourse.mybir import AluOpType as OP, ActivationFunctionType as AF
+
+R, N = 3, 4
+BIG = 1000000.0
+FAR = 2097152.0
+LANES = [(0, 64), (64, 112), (176, 48), (224, 32)]
+VL = 176
+SPLIT = 8
+
+SCRATCH = {}
+PLACE = {}
+PS = ["K0", "K1", "SM", "WB0", "WB1", "KN", "SUB0", "SUB1"]
+
+
+def _declare():
+    f, b, i, u = "float32", "bfloat16", "int32", "uint16"
+    sb = {}
+
+    def add(d, text):
+        for w in text.split():
+            k, n = w.split(":")
+            sb[k] = (int(n), d)
+
+    add(b, "xw:4352 dd:16640 qr:4096 qf0:256 qf1:256 q2:256 mmb:16 f0h:16 f2h:16 f2b:16 te:48 junk:256 cum:24 wb16:48 got:16 gv:256 cs:16 cc:16")
+    add(b, "bo:128 bw:144 bwf:144 pb:2048 rr:128 tri:128 sw:128 swi:128 idm:128 nid:128 dlt:16 ep:256 zz:256 lanep:256")
+    add(f, "pw:1288 mw:1024 th32:1 tb32:1 km:1024 kx:768 bm:256 bs:256 b1:256 li32:768 lim:768 wm:768 mn:768 uu:48 fc:64 nft:32 hit:48 tu:48 us:16")
+    add(f, "be:48 hb:48 ix:16 hm:16 m1:256 pm:256 kb:256 na:16 nb:16 nd:16 aa:16 ab:16 df:16 okd:16 sl:16 fin:16 gp:16 ud:48 fud:48 g48:48 so:48")
+    add(f, "ex:16 exd:16 xo:16 c3:16 came:16 t3:16 i3:16 oh:16 og:16 cg:16")
+    add(f, "colr:1 colp:1 colg:1 colg15:1 colr1:1 cole:1 colb:1 par:1 colsw:1 cold:1 colp16:1 mr:256 mf:256 mg:256 mask:256 bo32:128 bo256:128")
+    add(f, "mn0:256 mx0:256 sd0:256 one:16 lu:16 dp:48 dx:16 dn:16 bp:64")
+    add(i, "twi:1024 thi:1 u0i:16 mmi:16 ki:48 em:48 wi:48 wj:48 k3:16 e3:16 vi:256 vq:256 hv:256 ip:1 il:16 pr:1 pp:1 b4:16")
+    add(u, "us16:16 so16:48 xo16:16 i316:16 oh16:16 og16:16 li0:256 li1:256 li2:256 li3:256 uo0:16 uo1:16 uo2:16 uo3:16")
+    for t in range(R):
+        add(b, "xb%d:4096" % t)
+        add(f, "pb%d:1032" % t)
+    size = {}
+    for k, (n, d) in sb.items():
+        if n > 256 or k in ("qf0", "thi"):
+            SCRATCH[k] = ("sbuf", [128, n], d)
+            PLACE[k] = (k, 0, n)
+        else:
+            PLACE[k] = ("all_" + d, size.get(d, 0), n)
+            size[d] = size.get(d, 0) + (n + 15) // 16 * 16
+    for d in size:
+        SCRATCH["all_" + d] = ("sbuf", [128, size[d]], d)
+    for k in range(4):
+        SCRATCH["ring%d" % k] = ("sbuf", [128, LANES[k][1] // 16, 16, 16], b)
+    SCRATCH["mo8"] = ("sbuf", [8, 1024], i)
+    SCRATCH["mo8f"] = ("sbuf", [8, 1024], f)
+    SCRATCH["sel8"] = ("sbuf", [8, 128], f)
+    for k in PS:
+        SCRATCH[k] = ("psum", [128, 512], f)
+        PLACE[k] = (k, 0, 512)
+
+
+_declare()
+SEMAPHORES = ["sv", "sa", "st", "sg", "dq", "dx", "dt", "dh", "dm", "oy", "op", "om"] + ["%s%d" % (k, t) for k in ("ax", "ap", "lx", "lp") for t in range(R)]
+
+
+def rank_program(g, core, T, topo):
+    rank = T.rank_of(core)
+    if rank is None:
+        return
+    ENG = {"V": g.vector, "S": g.scalar, "P": g.tensor, "G": g, "Y": g.sync}
+    SEM = {"V": "sv", "S": "sa", "P": "st", "G": "sg"}
+    count, known, hist = {}, {q: {} for q in ENG}, {}
+
+    def wait_toks(q, toks):
+        need = {}
+        for (s, v, vc) in toks:
+            if known[q].get(s, 0) < v and need.get(s, (0, None))[0] < v:
+                need[s] = (v, vc)
+        for s in list(need):
+            if any(o != s and need[o][1].get(s, 0) >= need[s][0] for o in need):
+                del need[s]
+        for s in need:
+            ENG[q].wait_ge(T.sem[s], need[s][0])
+        for (s, v, vc) in toks:
+            for k in vc:
+                if known[q].get(k, 0) < vc[k]:
+                    known[q][k] = vc[k]
+
+    def deps(q, reads, writes):
+        out = []
+        for wr, regs in ((False, reads), (True, writes)):
+            for (b, lo, hi) in regs:
+                for (l, h, w, eq, tok) in hist.get(b, []):
+                    same = eq == q
+                    if b in PS and not same:
+                        out.append(tok)
+                    elif l < hi and lo < h and (w or wr):
+                        if same and (q == "P" or not w):
+                            continue
+                        out.append(tok)
+        return out
+
+    def note(eq, reads, writes, tok):
+        for (b, lo, hi) in writes:
+            hist[b] = [e for e in hist.get(b, []) if not (lo <= e[0] and e[1] <= hi)] + [(lo, hi, True, eq, tok)]
+        for (b, lo, hi) in reads:
+            hist[b] = [e for e in hist.get(b, []) if not (not e[2] and e[3] == eq and eq in SEM and lo <= e[0] and e[1] <= hi)] + [(lo, hi, False, eq, tok)]
+
+    def finish(q, sem, n, ins, reads, writes, eq):
+        count[sem] = count.get(sem, 0) + n
+        ins.then_inc(T.sem[sem], n)
+        vc = dict(known[q])
+        vc[sem] = count[sem]
+        note(eq, reads, writes, (sem, count[sem], vc))
+
+    def op(q, reads, writes, fn):
+        wait_toks(q, deps(q, reads, writes))
+        finish(q, SEM[q], 1, fn(), reads, writes, q)
+
+    def dma(sem, out, in_, reads, writes):
+        wait_toks("Y", deps("Y", reads, writes))
+        finish("Y", sem, 16, g.sync.dma_start(out, in_), reads, writes, "dma")
+
+    def C(name, a=0, b=None, st=1):
+        buf, at, n = PLACE[name]
+        b = n if b is None else b
+        return (T[buf][:, at + a:at + b:st] if st != 1 else T[buf][:, at + a:at + b], [(name, a, b)], [])
+
+    def U(name, s, n=1):
+        return C(name, 16 * s, 16 * s + 16 * n)
+
+    def PB(r):
+        return C("pb", 128 * r, 128 * r + 128)
+
+    def IND(w, o):
+        return (w[0].indirect(o[0]), w[1], o[1])
+
+    def rg(*xs):
+        return [r for x in xs if isinstance(x, tuple) for r in x[1] + x[2]]
+
+    def ap(x):
+        return x[0] if isinstance(x, tuple) else x
+
+    def tt(out, a, b, o):
+        op("V", rg(a, b) + out[2], out[1], lambda: g.vector.tensor_tensor(out[0], a[0], b[0], o))
+
+    def ts(out, a, s1, o1, s2=None, o2=None):
+        if o2 is None:
+            op("V", rg(a, s1), out[1], lambda: g.vector.tensor_scalar(out[0], a[0], ap(s1), None, o1))
+        else:
+            op("V", rg(a, s1, s2), out[1], lambda: g.vector.tensor_scalar(out[0], a[0], ap(s1), ap(s2), o1, o2))
+
+    def cp(out, a):
+        op("V", rg(a) + out[2], out[1], lambda: g.vector.tensor_copy(out[0], a[0]))
+
+    def fill(out, k):
+        op("V", [], out[1], lambda: g.vector.memset(out[0], k))
+
+    def scan(out, d0, d1, o0, o1):
+        op("V", rg(d0, d1), out[1], lambda: g.vector.tensor_tensor_scan(out[0], d0[0], d1[0], 0.0, o0, o1))
+
+    def act(out, a, func=AF.Copy, bias=None, scale=None, acc=None):
+        kw = {}
+        if bias is not None:
+            kw["bias"] = ap(bias)
+        if scale is not None:
+            kw["scale"] = ap(scale)
+        if acc is not None:
+            kw["accum_out"] = acc[0]
+        op("S", rg(a, bias, scale), out[1] + (acc[1] if acc is not None else []), lambda: g.scalar.activation(out[0], a[0], func, **kw))
+
+    def iota(x, pattern, start, by):
+        op("G", [], x[1], lambda: g.iota(x[0], pattern, start, by, allow_small_or_imprecise_dtypes=True))
+
+    def mms(lst):
+        def go():
+            for (o, l, r, a, b) in lst:
+                ins = g.tensor.matmul(o[0], l[0], r[0], a, b)
+            return ins
+        op("P", [x for m in lst for x in m[1][1] + m[2][1]], [x for m in lst for x in m[0][1]], go)
+
+    dma("dq", T["qf0"][:], T.qs[:], [], [("qf0", 0, 256)])
+    dma("dt", T["twi"][:], T.towns[:], [], [("twi", 0, 1024)])
+    dma("dx", T["xw"][:, 0:3904], T.x[:], [], [("xw", 0, 3904)])
+    dma("dh", T["thi"][:], T.th[:], [], [("thi", 0, 1)])
+    dma("dm", T["mo8"][:], T.mo[:], [], [("mo8", 0, 1024)])
+
+    iota(C("ip"), [[0, 1]], 0, 1)
+    iota(C("il"), [[16, 16]], 0, 1)
+    iota(C("mf"), [[1, 256]], 0, 0)
+    iota(C("mr"), [[0, 16], [1, 16]], 0, 0)
+    iota(C("mg"), [[16, 16], [0, 16]], 0, 0)
+    iota(C("ep"), [[0, 16], [1, 16]], 1, 0)
+    iota(C("lanep"), [[1, 256]], 0, 0)
+    ts(C("pr"), C("ip"), 15, OP.bitwise_and)
+    cp(C("colp"), C("ip"))
+    cp(C("colr"), C("pr"))
+    tt(C("colg"), C("colp"), C("colr"), OP.subtract)
+    ts(C("colr1"), C("colr"), 1.0, OP.add)
+    ts(C("colg15"), C("colg"), 15.0, OP.add)
+    ts(C("bwf"), C("mf", 0, 144), C("colg15"), OP.is_equal, C("colr1"), OP.mult)
+    ts(C("lu"), C("il"), C("colg"), OP.subtract)
+    ts(C("b4"), C("lu"), 4.0, OP.mult)
+    ts(C("bo"), C("mg", 0, 128), C("colg"), OP.is_equal)
+    ts(C("mask"), C("mr"), C("colr"), OP.is_equal)
+    ts(C("bw"), C("mf", 0, 144), C("colg15"), OP.is_equal, 32.0, OP.mult)
+    ts(C("idm"), C("mf", 0, 128), C("colp"), OP.is_equal)
+
+    def spread(qn, where):
+        for e in range(16):
+            if e % 2 == 0 and where == "S":
+                act(C("qr", e, 4096, 16), C(qn))
+            if e % 2 == 1 and where == "V":
+                cp(C("qr", e, 4096, 16), C(qn))
+
+    def starts(t, qn):
+        lst = [(C("SM", 0, 16), C("bwf", 15 - r, 143 - r), C(qn, r, 256, 16), r == 0, t == 0 and r == 15) for r in range(16)]
+        if t:
+            lst.append((C("SM", 0, 16), C("rr"), C("got"), False, True))
+        mms(lst)
+
+    def start_towns():
+        cp(C("u0i"), C("SM", 0, 16))
+        ts(C("mmi"), C("u0i"), 3, OP.bitwise_and)
+        tt(U("uu", 0), C("mmi"), C("b4"), OP.add)
+        cp(C("uo0"), U("uu", 0))
+
+    def entries(s, P):
+        cp(C("li%d" % s), IND(C(P, 0, 1024), C("uo%d" % s)))
+
+    starts(0, "qf0")
+    for e in range(16):
+        act(C("qr", e, 4096, 16), C("qf0"))
+    act(C("nid"), C("idm"), AF.Copy, None, -1.0)
+    cp(C("pw", 0, 1024), C("twi"))
+    start_towns()
+    entries(0, "pw")
+    fill(C("xw", 3904, 4096), 0.0)
+    fill(C("pw", 1024, 1032), 0.0)
+    cp(C("pw", 1024, 1025), C("thi"))
+
+    def constants():
+        for r in range(16):
+            if r % 2:
+                act(PB(r), C("bo"), AF.Identity, None, C("mask", r, r + 1))
+            else:
+                ts(PB(r), C("bo"), C("mask", r, r + 1), OP.mult)
+        ts(C("th32"), C("thi"), 32.0, OP.mult)
+        ts(C("mn0"), C("mr"), 0.0, OP.is_equal, 2.0 * BIG, OP.mult)
+        ts(C("mn0"), C("mn0"), -BIG, OP.add)
+        ts(C("sd0"), C("mr"), 0.0, OP.not_equal)
+        ts(C("mx0"), C("mr"), 0.0, OP.is_equal, -BIG, OP.mult)
+        ts(C("mx0"), C("mx0"), 2.0, OP.add)
+        fill(C("dd", 16384 + VL, 16640), 0.0)
+
+    def late_constants():
+        ts(C("pp"), C("ip"), 1, OP.bitwise_and)
+        cp(C("par"), C("pp"))
+        ts(C("cole"), C("colr"), -1.0, OP.mult, 31.0, OP.add)
+        ts(C("colb"), C("colr"), 64.0, OP.mult, -1984.0, OP.add)
+        ts(C("colsw"), C("par"), -2.0, OP.mult, 1.0, OP.add)
+        ts(C("cold"), C("par"), -8.0, OP.mult, 4.0, OP.add)
+        tt(C("colsw"), C("colsw"), C("colp"), OP.add)
+        ts(C("tri"), C("mr", 0, 128), C("colr"), OP.is_gt)
+        tt(C("tri"), C("tri"), C("bo"), OP.mult)
+        ts(C("sw"), C("mf", 0, 128), C("colsw"), OP.is_equal)
+        tt(C("swi"), C("sw"), C("idm"), OP.subtract)
+        ts(C("dlt"), C("mr", 0, 16), 0.0, OP.mult, C("cold"), OP.add)
+        act(C("rr"), C("mask", 0, 128))
+        ts(C("bo32"), C("mg", 0, 128), C("colg"), OP.is_equal)
+        act(C("bo256"), C("bo32"), AF.Copy, None, 256.0)
+        fill(C("one"), 1.0)
+        fill(C("fc", 0, 16), 1.0)
+        fill(C("cum"), 0.0)
+        fill(C("zz"), 0.0)
+        for s in range(3):
+            act(U("dp", s), C("lu"), AF.Copy, 1032.0)
+        act(C("dx"), C("lu"), AF.Copy, 4096.0)
+        act(C("dn"), C("lu"), AF.Copy, 16384.0)
+        for s in range(4):
+            act(U("bp", s), C("lu"), AF.Copy, 4096.0 * s - 16385.0, 15.0)
+
+    def load_mothers():
+        cp((T["mo8f"][:, :], [("mo8f", 0, 1024)], []), (T["mo8"][:, :], [("mo8", 0, 1024)], []))
+        ts(C("colp16"), C("colp"), 16.0, OP.mult)
+        bm, am, _ = PLACE["mg"]
+        bc, ac, _ = PLACE["colp16"]
+        op("V", [("mg", 0, 128), ("colp16", 0, 1)], [("sel8", 0, 128)], lambda: g.vector.tensor_scalar(T["sel8"][:, :], T[bm][0:8, am:am + 128], T[bc][0:8, ac:ac + 1], None, OP.is_equal))
+        for h, b in ((0, "WB0"), (1, "WB1")):
+            mms([(C(b), (T["sel8"][:, :], [("sel8", 0, 128)], []), (T["mo8f"][:, 512 * h:512 * h + 512], [("mo8f", 0, 1024)], []), True, True)])
+
+    def keep_mothers():
+        for h, b in ((0, "WB0"), (1, "WB1")):
+            act(C("mw", 512 * h, 512 * h + 512), C(b))
+
+    def send(t):
+        dst, frm = T.cores[(rank - 1 - t) % N], T.cores[(rank + 1 + t) % N]
+        rid, pid, _ = topo.addr(dst)
+        for kind, src, dest, n in (("p", "pw", "pb%d" % t, 1032), ("x", "xw", "xb%d" % t, 4096)):
+            wait_toks("G", deps("G", [(src, 0, n)], []))
+            asem, lsem = "a%s%d" % (kind, t), "l%s%d" % (kind, t)
+            g.remote_dma(T[dest][:, 0:n], T[src][:, 0:n], T.sem[asem], T.sem[lsem], pid, rid, topo.mask(core, dst))
+            count[lsem] = len(topo.engines(core, dst))
+            vc = dict(known["G"])
+            vc[lsem] = count[lsem]
+            note("dma", [(src, 0, n)], [], (lsem, count[lsem], vc))
+            count[asem] = len(topo.engines(frm, core))
+            note("dma", [], [(dest, 0, n)], (asem, count[asem], {asem: count[asem]}))
+
+    def mother(s):
+        tt(C("bm"), IND(C("mw"), C("uo%d" % s)), C("mask"), OP.mult)
+        scan(C("bs"), C("sd0"), C("bm"), OP.mult, OP.add)
+        cp(C("uo%d" % (s + 1)), C("bs", 15, 256, 16))
+        if s < 2:
+            act(U("uu", s + 1), C("bs", 15, 256, 16))
+
+    def dcols(s, k):
+        a, n = LANES[k]
+        return C("dd", 4096 * s + 16 * a, 4096 * s + 16 * (a + n))
+
+    def ring(k, h=None):
+        n, c = "ring%d" % k, LANES[k][1] // 16
+        if h is None:
+            return (T[n][:, :, :, :], [(n, 0, 256 * c)], [])
+        lo, hi = (0, (c + 1) // 2) if h == 0 else ((c + 1) // 2, c)
+        return (T[n][:, lo:hi, :, :], [(n, 256 * lo, 256 * hi)], [], 256 * lo, 256 * hi)
+
+    def got_from(s, k, X):
+        a, n = LANES[k]
+        return IND(C(X, 0, 4096), C("li%d" % s, a, a + n))
+
+    def vget(s, k, X):
+        a, n = LANES[k]
+        tt(dcols(s, k), got_from(s, k, X), C("qr", 16 * a, 16 * (a + n)), OP.subtract)
+
+    def sget(s, k, X):
+        act(dcols(s, k), got_from(s, k, X))
+
+    def ssub(s, k):
+        for h in range(2):
+            lo, hi = ring(k, h)[3:]
+            a = 16 * LANES[k][0]
+            o = C("SUB%d" % h, 0, hi - lo)
+            mms([(o, C("nid"), C("qr", a + lo, a + hi), True, False), (o, C("idm"), C("dd", 4096 * s + a + lo, 4096 * s + a + hi), False, True)])
+
+    def vabs(s, k):
+        act(ring(k), dcols(s, k), AF.Abs)
+
+    def sabs(s, k):
+        for h in range(2):
+            r = ring(k, h)
+            act(r[:3], C("SUB%d" % h, 0, r[4] - r[3]), AF.Abs)
+
+    def dist(s, k):
+        a, n = LANES[k]
+        o = C("K%d" % (s % 2), a, a + n)
+        rn = "ring%d" % k
+        mms([(o, PB(0), C("ep", 0, n), True, False)] + [(o, C("bw", 15 - r, 143 - r), (T[rn][:, :, r, :], [(rn, 0, 16 * n)], []), False, r == 15) for r in range(16)])
+
+    def sA(s, X):
+        if s:
+            sget(s, 2, X)
+            ssub(s, 2)
+        vabs(s, 0)
+        dist(s, 0)
+        sget(s, 3, X)
+        sabs(s, 2)
+        ssub(s, 3)
+        dist(s, 2)
+
+    def sB(s):
+        vabs(s, 1)
+        dist(s, 1)
+        sabs(s, 3)
+        dist(s, 3)
+
+    def minscan(s):
+        scan(C("km", 256 * s, 256 * s + 256), C("mn0"), C("K%d" % (s % 2), 0, 256), OP.max, OP.min)
+
+    def maxscan(s):
+        scan(C("kx", 256 * s, 256 * s + 256), C("mx0"), C("K%d" % (s % 2), 0, 256), OP.add, OP.max)
+
+    def bcast(bank, at, srcs, whole):
+        return [(C(bank, at + r, at + 256, 16), PB(r), src, whole and i == 0, whole and i == len(srcs) - 1) for r in range(16) for i, src in enumerate(srcs)]
+
+    def worst2(lo, n, bank):
+        a, b = 256 * lo, 256 * (lo + n)
+        ts(C("wm", a, b), C(bank, 0, 256 * n), C("cole"), OP.is_equal)
+        act(C(bank, 0, 256 * n), C(bank, 0, 256 * n), AF.Square, C("colb"), 64.0)
+        tt(C("lim", a, b), C("li32", a, b), C(bank, 0, 256 * n), OP.min)
+
+    for t in range(R):
+        last = t == R - 1
+        split = 13 if last else SPLIT
+        q, qn = "qf%d" % (t % 2), "qf%d" % ((t + 1) % 2)
+        X3, P3 = "xb%d" % t, "pb%d" % t
+        if t:
+            entries(0, "pw")
+        vget(0, 0, "xw")
+        sget(0, 2, "xw")
+        ssub(0, 2)
+        if t == 0:
+            constants()
+            load_mothers()
+        vget(0, 1, "xw")
+        if t == 0:
+            send(0)
+        sA(0, "xw")
+        if t == 0:
+            keep_mothers()
+            late_constants()
+        mother(0)
+        entries(1, "pw")
+        vget(1, 0, "xw")
+        sB(0)
+        mother(1)
+        entries(2, "pw")
+        vget(1, 1, "xw")
+        act(C("b1"), IND(C("mw"), C("uo0")))
+        cp(C("mmb"), C("mmi"))
+        mother(2)
+        minscan(0)
+        maxscan(0)
+        sA(1, "xw")
+        ts(U("fc", 1), C("km", 15, 256, 16), C("th32"), OP.is_ge)
+        cp(C("f0h"), U("fc", 1))
+        act(C("li32", 0, 256), IND(C("pw", 0, 1024), C("uo0")))
+        sB(1)
+        mms([(C("SM", 16, 32), C("sw"), C("f0h"), True, True), (C("SM", 32, 48), C("swi"), C("mmb"), True, False), (C("SM", 32, 48), C("idm"), C("dlt"), False, True)])
+        vget(2, 0, "xw")
+        vget(2, 1, "xw")
+        act(C("li32", 256, 512), IND(C("pw", 0, 1024), C("uo1")))
+        minscan(1)
+        maxscan(1)
+        sA(2, "xw")
+        tt(C("ex"), U("fc", 1), C("SM", 16, 32), OP.mult)
+        tt(C("exd"), C("ex"), C("SM", 32, 48), OP.mult)
+        tt(C("xo"), C("exd"), U("uu", 0), OP.add)
+        cp(C("xo16"), C("xo"))
+        cp(IND(C("mw"), C("xo16")), C("b1"))
+        if last:
+            dma("om", T.ym[:], T["mw"][0:128:16, :], [("mw", 0, 1024)], [])
+        act(C("li32", 512, 768), IND(C("pw", 0, 1024), C("uo2")))
+        cp(U("wi", 0, 2), C("kx", 15, 512, 16))
+        ts(U("wj", 0, 2), U("wi", 0, 2), 31, OP.bitwise_and)
+        cp(U("wb16", 0, 2), U("wj", 0, 2))
+        mms(bcast("WB0", 0, [U("wb16", 0)], True) + bcast("WB0", 256, [U("wb16", 1)], True))
+        sB(2)
+        entries(3, P3)
+        vget(3, 0, X3)
+        tt(C("ud"), C("uu"), C("dp"), OP.subtract)
+        worst2(0, 2, "WB0")
+        act(C("tb32"), C(P3, 1024, 1025), AF.Copy, None, 32.0)
+        sget(3, 2, X3)
+        ssub(3, 2)
+        minscan(2)
+        ts(C("nft"), C("km", 271, 768, 16), C("th32"), OP.is_ge)
+        cp(C("ki"), C("km", 15, 768, 16))
+        tt(U("fc", 2), U("fc", 1), U("nft", 0), OP.mult)
+        ts(C("em"), C("ki"), 31, OP.bitwise_and)
+        tt(U("fc", 3), U("fc", 2), U("nft", 1), OP.mult)
+        tt(C("hit"), U("fc", 0, 3), U("fc", 1, 3), OP.subtract)
+        scan(C("cum", 1, 17), C("one"), U("fc", 3), OP.mult, OP.add)
+        tt(C("te"), C("hit"), C("em"), OP.mult)
+        tt(C("tu"), C("hit"), C("uu"), OP.mult)
+        tt(U("te", 0), U("te", 0), U("te", 1), OP.add)
+        tt(C("us"), U("tu", 0), U("tu", 1), OP.add)
+        tt(U("te", 0), U("te", 0), U("te", 2), OP.add)
+        tt(C("us"), C("us"), U("tu", 2), OP.add)
+        mms(bcast("SM", 256, [U("te", 0)], True))
+        cp(C("us16"), C("us"))
+        cp(C("f2h"), U("fc", 3))
+        ts(C("f2b"), U("fc", 3), FAR, OP.mult)
+        mms([(C("SM", 48, 64), C("bo"), C("cum", 0, 16), True, False), (C("SM", 48, 64), C("tri"), C("f2h"), False, True)])
+        sget(3, 3, X3)
+        sabs(3, 2)
+        ssub(3, 3)
+        dist(3, 2)
+        maxscan(2)
+        ts(C("m1"), C("SM", 256, 512), C("colr1"), OP.is_equal)
+        cp(C("sl"), C("SM", 48, 64))
+        tt(C("pm"), IND(C("pw", 0, 1024), C("us16")), C("m1"), OP.mult)
+        mms([(C("KN", 0, 256), C("bo256"), C("pm"), True, False)] + bcast("KN", 0, [C("f2b")], False) + [(C("KN", 0, 256), PB(0), C("lanep"), False, True)])
+        cp(U("wi", 2), C("kx", 527, 768, 16))
+        ts(U("wj", 2), U("wi", 2), 31, OP.bitwise_and)
+        cp(U("wb16", 2), U("wj", 2))
+        vabs(3, 0)
+        dist(3, 0)
+        sabs(3, 3)
+        vget(3, 1, X3)
+        mms(bcast("WB1", 0, [U("wb16", 2)], True))
+        dist(3, 3)
+        vabs(3, 1)
+        dist(3, 1)
+        tt(C("bm"), C("KN", 0, 256), C("mask"), OP.mult)
+        act(C("kb"), C("KN", 0, 256))
+        mms([(C("KN", 256, 512), C("bo32"), C("pm"), True, False)])
+        scan(C("bs"), C("sd0"), C("bm"), OP.mult, OP.add)
+        act(C("na"), C("bs", 15, 256, 16), AF.Copy, 0.5, -1.0)
+        ts(C("hm"), U("fc", 3), -1.0, OP.mult, 1.0, OP.add)
+        worst2(2, 1, "WB1")
+        tt(C("be"), C("em"), U("bp", 0, 3), OP.add)
+        ts(C("fin"), C("sl"), 64.0, OP.is_lt)
+        tt(C("hb"), C("hit"), C("be"), OP.mult)
+        tt(C("fin"), C("fin"), U("fc", 3), OP.mult)
+        tt(C("ix"), U("hb", 0), U("hb", 1), OP.add)
+        ts(C("gp"), C("sl"), 3904.0 + 64 * t, OP.add)
+        tt(C("ix"), C("ix"), U("hb", 2), OP.add)
+        tt(C("fud"), U("fc", 1, 3), C("ud"), OP.mult)
+        tt(C("ix"), C("ix"), C("dn"), OP.add)
+        tt(C("gp"), C("gp"), C("dx"), OP.subtract)
+        act(C("dd", 16384, 16384 + VL), C(q, 0, VL), AF.Copy, None, -1.0)
+        act(C("q2", 0, VL), C(q, 0, VL), AF.Copy, None, 2.0)
+        act(C("q2", VL, 256), C(q, VL, 256))
+        tt(C("nb"), C("na"), C("lu"), OP.add)
+        ts(C("nd"), C("nb"), 0.5, OP.subtract, -1.0 / 256, OP.mult)
+        tt(C("nd"), C("nd"), C("dx"), OP.subtract)
+
+        def lowest(c0, c1):
+            for c in range(c0, c1):
+                for k, o in (("na", "aa"), ("nb", "ab")):
+                    act(C("junk", 0, 16 * c + 16), C("kb", 0, 16 * c + 16), AF.Sign, C(k, c, c + 1), None, C(o, c, c + 1))
+
+        lowest(0, split)
+        minscan(3)
+        ts(C("c3"), C("km", 783, 1024, 16), C("tb32"), OP.is_lt)
+        cp(C("k3"), C("km", 783, 1024, 16))
+        tt(C("came"), C("c3"), C("fin"), OP.mult)
+        ts(C("e3"), C("k3"), 31, OP.bitwise_and)
+        tt(C("got"), C("came"), C("hm"), OP.add)
+        tt(C("t3"), C("e3"), U("bp", 3), OP.add)
+        tt(C("cs"), C("came"), C("sl"), OP.mult)
+        tt(C("i3"), C("t3"), C("came"), OP.mult)
+        act(C("cc"), C("came"), AF.Copy, None, 3904.0 + 64 * t)
+        for s in range(3):
+            act(U("g48", s), C("got"))
+        mms(bcast("KN", 256, [C("cs"), C("cc")], False) + [(C("KN", 256, 512), PB(0), C("zz"), False, True)])
+        tt(C("i3"), C("i3"), C("ix"), OP.add)
+        cp(C("i316"), C("i3"))
+        tt(C("cg"), C("came"), C("gp"), OP.mult)
+        tt(C("vi"), IND(C("dd"), C("i316")), C("q2"), OP.add)
+        tt(C("og"), C("cg"), C("dx"), OP.add)
+        if not last:
+            ts(C("vq"), C("vi"), 255, OP.bitwise_and)
+        cp(C("og16"), C("og"))
+        if not last:
+            cp(C(qn), C("vq"))
+            starts(t + 1, qn)
+            spread(qn, "S")
+        lowest(split, 16)
+        tt(C("gv"), C("vi"), C(q), OP.subtract)
+        ts(C("hv"), C("vi"), 1, OP.arith_shift_right)
+        cp(IND(C("xw"), C("og16")), C("gv"))
+
+        def lists():
+            tt(C("so"), C("fud"), C("g48"), OP.mult)
+            for s in (2, 1, 0):
+                tt(C("mn", 256 * s, 256 * s + 256), C("KN", 256, 512), C("wm", 256 * s, 256 * s + 256), OP.mult)
+                if s == 2:
+                    tt(C("so"), C("so"), C("dp"), OP.add)
+                if s == 1:
+                    cp(C("so16"), C("so"))
+            for s in (2, 1, 0):
+                a, b = 256 * s, 256 * s + 256
+                tt(IND(C("pw"), U("so16", s)), C("lim", a, b), C("mn", a, b), OP.add)
+
+        def records():
+            tt(C("df"), C("ab"), C("aa"), OP.subtract)
+            ts(C("okd"), C("df"), 1.0, OP.is_lt)
+            tt(C("okd"), C("okd"), C("hm"), OP.mult)
+            tt(C("oh"), C("okd"), C("nd"), OP.mult)
+            tt(C("oh"), C("oh"), C("dx"), OP.add)
+            cp(C("oh16"), C("oh"))
+            cp(IND(C("xw"), C("oh16")), C("hv"))
+
+        if last:
+            records()
+            dma("oy", T.yx[:], T["xw"][:, 0:4096], [("xw", 0, 4096)], [])
+            lists()
+            dma("op", T.yp[:], T["pw"][:, 0:1024], [("pw", 0, 1024)], [])
+        else:
+            lists()
+            start_towns()
+            spread(qn, "V")
+            records()
+            send(t + 1)
+
+    for s in count:
+        if known["G"].get(s, 0) < count[s]:
+            g.wait_ge(T.sem[s], count[s])

@@ -5,7 +5,9 @@ BIG = 1000000.0
 FAR = 2097152.0
 LANES = [(0, 64), (64, 112), (176, 48), (224, 32)]
 VL = 176
-SPLIT = 8
+SPLIT0, SPLIT, PART = 4, 11, 64
+POOL, VEC = (1, 5, 9, 13), (3, 11)
+LEAST, MOST = [0, 256, 512, 1536], [1024, 1280, 768]
 
 SCRATCH = {}
 PLACE = {}
@@ -22,13 +24,13 @@ def _declare():
             sb[k] = (int(n), d)
 
     add(b, "xw:4352 dd:16640 qr:4096 qf0:256 qf1:256 q2:256 mmb:16 f0h:16 f2h:16 f2b:16 te:48 junk:256 cum:24 wb16:48 got:16 gv:256 cs:16 cc:16")
-    add(b, "bo:128 bw:144 bwf:144 pb:2048 rr:128 tri:128 sw:128 swi:128 idm:128 nid:128 dlt:16 ep:256 zz:256 lanep:256")
-    add(f, "pw:1288 mw:1024 th32:1 tb32:1 km:1024 kx:768 bm:256 bs:256 b1:256 li32:768 lim:768 wm:768 mn:768 uu:48 fc:64 nft:32 hit:48 tu:48 us:16")
-    add(f, "be:48 hb:48 ix:16 hm:16 m1:256 pm:256 kb:256 na:16 nb:16 nd:16 aa:16 ab:16 df:16 okd:16 sl:16 fin:16 gp:16 ud:48 fud:48 g48:48 so:48")
+    add(b, "bo:128 bw:144 bwf:144 pb:2048 rr:128 tri:128 sw:128 swi:128 idm:128 nid:128 dlt:16 lub:16 gcs:48 ep:256 zz:256 lanep:256")
+    add(f, "pw:1288 mw:1024 th32:1 tb32:1 km:1792 bm:256 bs:256 b1:256 li32:768 lim:768 wm:768 mn:768 uu:48 fc:64 nft:32 hit:48 tu:48 us:16")
+    add(f, "be:48 hb:48 hm:16 m1:256 pm:256 kb:256 na:16 nb:16 nd:16 aa:16 ab:16 okd:16 fin:16 ud:48 fud:48 g48:48 so:48")
     add(f, "ex:16 exd:16 xo:16 c3:16 came:16 t3:16 i3:16 oh:16 og:16 cg:16")
-    add(f, "colr:1 colp:1 colg:1 colg15:1 colr1:1 cole:1 colb:1 par:1 colsw:1 cold:1 colp16:1 mr:256 mf:256 mg:256 mask:256 bo32:128 bo256:128")
+    add(f, "colr:1 colp:1 colg:1 colg15:1 colr1:1 cole:1 colb:1 par:1 colsw:1 cold:1 colp16:1 mr:256 mf:256 mg:256 mask:256 bo32:128 bo256:128 idm32:128")
     add(f, "mn0:256 mx0:256 sd0:256 one:16 lu:16 dp:48 dx:16 dn:16 bp:64")
-    add(i, "twi:1024 thi:1 u0i:16 mmi:16 ki:48 em:48 wi:48 wj:48 k3:16 e3:16 vi:256 vq:256 hv:256 ip:1 il:16 pr:1 pp:1 b4:16")
+    add(i, "twi:1024 thi:1 u0i:16 mmi:16 ki:64 em:64 wi:48 wj:48 k3:16 e3:16 vi:256 vq:256 hv:256 ip:1 il:16 pr:1 pp:1 b4:16")
     add(u, "us16:16 so16:48 xo16:16 i316:16 oh16:16 og16:16 li0:256 li1:256 li2:256 li3:256 uo0:16 uo1:16 uo2:16 uo3:16")
     for t in range(R):
         add(b, "xb%d:4096" % t)
@@ -43,8 +45,8 @@ def _declare():
             size[d] = size.get(d, 0) + (n + 15) // 16 * 16
     for d in size:
         SCRATCH["all_" + d] = ("sbuf", [128, size[d]], d)
-    for k in range(4):
-        SCRATCH["ring%d" % k] = ("sbuf", [128, LANES[k][1] // 16, 16, 16], b)
+    for k in range(3):
+        SCRATCH["ring%d" % k] = ("sbuf", [128, (LANES[k][1] if k < 2 else 256 - VL) // 16, 16, 16], b)
     SCRATCH["mo8"] = ("sbuf", [8, 1024], i)
     SCRATCH["mo8f"] = ("sbuf", [8, 1024], f)
     SCRATCH["sel8"] = ("sbuf", [8, 128], f)
@@ -118,6 +120,8 @@ def rank_program(g, core, T, topo):
     def C(name, a=0, b=None, st=1):
         buf, at, n = PLACE[name]
         b = n if b is None else b
+        if name == "qr":
+            return (T[buf][:, a:b:st], [("qr", a, a + 1)], []) if st == 16 else (T[buf][:, a:b], [("qr", 0, 16)], [])
         return (T[buf][:, at + a:at + b:st] if st != 1 else T[buf][:, at + a:at + b], [(name, a, b)], [])
 
     def U(name, s, n=1):
@@ -202,10 +206,15 @@ def rank_program(g, core, T, topo):
 
     def spread(qn, where):
         for e in range(16):
-            if e % 2 == 0 and where == "S":
-                act(C("qr", e, 4096, 16), C(qn))
-            if e % 2 == 1 and where == "V":
-                cp(C("qr", e, 4096, 16), C(qn))
+            o = C("qr", e, 4096, 16)
+            if e in POOL:
+                if where == "G":
+                    op("G", [(qn, 0, 256)], o[1], lambda: g.affine_select(o[0], C(qn)[0], [[0, 256]], OP.is_ge, 0.0, 0, 0))
+            elif e in VEC:
+                if where == "V":
+                    cp(o, C(qn))
+            elif where == "S":
+                act(o, C(qn))
 
     def starts(t, qn):
         lst = [(C("SM", 0, 16), C("bwf", 15 - r, 143 - r), C(qn, r, 256, 16), r == 0, t == 0 and r == 15) for r in range(16)]
@@ -262,6 +271,10 @@ def rank_program(g, core, T, topo):
         ts(C("dlt"), C("mr", 0, 16), 0.0, OP.mult, C("cold"), OP.add)
         act(C("rr"), C("mask", 0, 128))
         ts(C("bo32"), C("mg", 0, 128), C("colg"), OP.is_equal)
+        act(C("idm32"), C("idm"))
+        act(C("lub"), C("lu"))
+        for s in range(R):
+            act(U("gcs", s), C("lu"), AF.Copy, 64.0 * s - 192.0, 0.0)
         act(C("bo256"), C("bo32"), AF.Copy, None, 256.0)
         fill(C("one"), 1.0)
         fill(C("fc", 0, 16), 1.0)
@@ -312,44 +325,48 @@ def rank_program(g, core, T, topo):
         a, n = LANES[k]
         return C("dd", 4096 * s + 16 * a, 4096 * s + 16 * (a + n))
 
-    def ring(k, h=None):
-        n, c = "ring%d" % k, LANES[k][1] // 16
-        if h is None:
-            return (T[n][:, :, :, :], [(n, 0, 256 * c)], [])
+    def half(k, h):
+        c = LANES[k][1] // 16
         lo, hi = (0, (c + 1) // 2) if h == 0 else ((c + 1) // 2, c)
-        return (T[n][:, lo:hi, :, :], [(n, 256 * lo, 256 * hi)], [], 256 * lo, 256 * hi)
+        o = LANES[2][1] // 16 if k == 3 else 0
+        return (T["ring2"][:, o + lo:o + hi, :, :], [("ring2", 256 * (o + lo), 256 * (o + hi))], []), 256 * lo, 256 * hi
 
-    def got_from(s, k, X):
-        a, n = LANES[k]
-        return IND(C(X, 0, 4096), C("li%d" % s, a, a + n))
+    def vpart(s, a, n, X):
+        tt(C("dd", 4096 * s + 16 * a, 4096 * s + 16 * (a + n)), IND(C(X, 0, 4096), C("li%d" % s, a, a + n)), C("qr", 16 * a, 16 * (a + n)), OP.subtract)
 
     def vget(s, k, X):
-        a, n = LANES[k]
-        tt(dcols(s, k), got_from(s, k, X), C("qr", 16 * a, 16 * (a + n)), OP.subtract)
+        vpart(s, LANES[k][0], LANES[k][1], X)
 
     def sget(s, k, X):
-        act(dcols(s, k), got_from(s, k, X))
+        a, n = LANES[k]
+        act(dcols(s, k), IND(C(X, 0, 4096), C("li%d" % s, a, a + n)))
 
     def ssub(s, k):
         for h in range(2):
-            lo, hi = ring(k, h)[3:]
+            _, lo, hi = half(k, h)
             a = 16 * LANES[k][0]
             o = C("SUB%d" % h, 0, hi - lo)
             mms([(o, C("nid"), C("qr", a + lo, a + hi), True, False), (o, C("idm"), C("dd", 4096 * s + a + lo, 4096 * s + a + hi), False, True)])
 
-    def vabs(s, k):
-        act(ring(k), dcols(s, k), AF.Abs)
+    def vabs(s, k, c0=0, c1=None):
+        c1 = LANES[k][1] // 16 if c1 is None else c1
+        n, a = "ring%d" % k, 4096 * s + 16 * LANES[k][0]
+        act((T[n][:, c0:c1, :, :], [(n, 256 * c0, 256 * c1)], []), C("dd", a + 256 * c0, a + 256 * c1), AF.Abs)
 
     def sabs(s, k):
         for h in range(2):
-            r = ring(k, h)
-            act(r[:3], C("SUB%d" % h, 0, r[4] - r[3]), AF.Abs)
+            r, lo, hi = half(k, h)
+            act(r, C("SUB%d" % h, 0, hi - lo), AF.Abs)
 
-    def dist(s, k):
-        a, n = LANES[k]
+    def dist(s, k, c0=0, c1=None):
+        c1 = LANES[k][1] // 16 if c1 is None else c1
+        a, n = LANES[k][0] + 16 * c0, 16 * (c1 - c0)
         o = C("K%d" % (s % 2), a, a + n)
         rn = "ring%d" % k
-        mms([(o, PB(0), C("ep", 0, n), True, False)] + [(o, C("bw", 15 - r, 143 - r), (T[rn][:, :, r, :], [(rn, 0, 16 * n)], []), False, r == 15) for r in range(16)])
+        mms([(o, PB(0), C("ep", 0, n), True, False)] + [(o, C("bw", 15 - r, 143 - r), (T[rn][:, c0:c1, r, :], [(rn, 256 * c0, 256 * c1)], []), False, r == 15) for r in range(16)])
+
+    def sdist(s):
+        dist(s, 2, 0, (256 - VL) // 16)
 
     def sA(s, X):
         if s:
@@ -360,32 +377,25 @@ def rank_program(g, core, T, topo):
         sget(s, 3, X)
         sabs(s, 2)
         ssub(s, 3)
-        dist(s, 2)
 
     def sB(s):
         vabs(s, 1)
         dist(s, 1)
         sabs(s, 3)
-        dist(s, 3)
+        sdist(s)
 
     def minscan(s):
-        scan(C("km", 256 * s, 256 * s + 256), C("mn0"), C("K%d" % (s % 2), 0, 256), OP.max, OP.min)
+        scan(C("km", LEAST[s], LEAST[s] + 256), C("mn0"), C("K%d" % (s % 2), 0, 256), OP.max, OP.min)
 
     def maxscan(s):
-        scan(C("kx", 256 * s, 256 * s + 256), C("mx0"), C("K%d" % (s % 2), 0, 256), OP.add, OP.max)
+        scan(C("km", MOST[s], MOST[s] + 256), C("mx0"), C("K%d" % (s % 2), 0, 256), OP.add, OP.max)
 
     def bcast(bank, at, srcs, whole):
         return [(C(bank, at + r, at + 256, 16), PB(r), src, whole and i == 0, whole and i == len(srcs) - 1) for r in range(16) for i, src in enumerate(srcs)]
 
-    def worst2(lo, n, bank):
-        a, b = 256 * lo, 256 * (lo + n)
-        ts(C("wm", a, b), C(bank, 0, 256 * n), C("cole"), OP.is_equal)
-        act(C(bank, 0, 256 * n), C(bank, 0, 256 * n), AF.Square, C("colb"), 64.0)
-        tt(C("lim", a, b), C("li32", a, b), C(bank, 0, 256 * n), OP.min)
-
     for t in range(R):
         last = t == R - 1
-        split = 13 if last else SPLIT
+        split = 16 if last else SPLIT
         q, qn = "qf%d" % (t % 2), "qf%d" % ((t + 1) % 2)
         X3, P3 = "xb%d" % t, "pb%d" % t
         if t:
@@ -435,7 +445,7 @@ def rank_program(g, core, T, topo):
         if last:
             dma("om", T.ym[:], T["mw"][0:128:16, :], [("mw", 0, 1024)], [])
         act(C("li32", 512, 768), IND(C("pw", 0, 1024), C("uo2")))
-        cp(U("wi", 0, 2), C("kx", 15, 512, 16))
+        cp(U("wi", 0, 2), C("km", 1039, 1536, 16))
         ts(U("wj", 0, 2), U("wi", 0, 2), 31, OP.bitwise_and)
         cp(U("wb16", 0, 2), U("wj", 0, 2))
         mms(bcast("WB0", 0, [U("wb16", 0)], True) + bcast("WB0", 256, [U("wb16", 1)], True))
@@ -443,19 +453,22 @@ def rank_program(g, core, T, topo):
         entries(3, P3)
         vget(3, 0, X3)
         tt(C("ud"), C("uu"), C("dp"), OP.subtract)
-        worst2(0, 2, "WB0")
+        ts(C("wm", 0, 512), C("WB0"), C("cole"), OP.is_equal)
+        act(C("WB0"), C("WB0"), AF.Square, C("colb"), 64.0)
+        tt(C("lim", 0, 512), C("li32", 0, 512), C("WB0"), OP.min)
         act(C("tb32"), C(P3, 1024, 1025), AF.Copy, None, 32.0)
         sget(3, 2, X3)
         ssub(3, 2)
         minscan(2)
+        maxscan(2)
         ts(C("nft"), C("km", 271, 768, 16), C("th32"), OP.is_ge)
-        cp(C("ki"), C("km", 15, 768, 16))
+        cp(C("ki"), C("km", 15, 1024, 16))
         tt(U("fc", 2), U("fc", 1), U("nft", 0), OP.mult)
         ts(C("em"), C("ki"), 31, OP.bitwise_and)
         tt(U("fc", 3), U("fc", 2), U("nft", 1), OP.mult)
         tt(C("hit"), U("fc", 0, 3), U("fc", 1, 3), OP.subtract)
         scan(C("cum", 1, 17), C("one"), U("fc", 3), OP.mult, OP.add)
-        tt(C("te"), C("hit"), C("em"), OP.mult)
+        tt(C("te"), C("hit"), U("em", 0, 3), OP.mult)
         tt(C("tu"), C("hit"), C("uu"), OP.mult)
         tt(U("te", 0), U("te", 0), U("te", 1), OP.add)
         tt(C("us"), U("tu", 0), U("tu", 1), OP.add)
@@ -464,74 +477,76 @@ def rank_program(g, core, T, topo):
         mms(bcast("SM", 256, [U("te", 0)], True))
         cp(C("us16"), C("us"))
         cp(C("f2h"), U("fc", 3))
-        ts(C("f2b"), U("fc", 3), FAR, OP.mult)
         mms([(C("SM", 48, 64), C("bo"), C("cum", 0, 16), True, False), (C("SM", 48, 64), C("tri"), C("f2h"), False, True)])
+        mms([(C("SM", 80, 96), l, x, i == 0, i == 3) for i, (l, x) in enumerate([(C("bo"), C("cum", 0, 16)), (C("tri"), C("f2h")), (C("nid"), C("lub")), (C("idm"), U("gcs", t))])])
         sget(3, 3, X3)
+        act(C("f2b"), U("fc", 3), AF.Copy, None, FAR)
+        act(C("hm"), U("fc", 3), AF.Copy, 1.0, -1.0)
+        mms([(C("KN", 0, 256), PB(0), C("lanep"), True, False)] + bcast("KN", 0, [C("f2b")], False))
         sabs(3, 2)
         ssub(3, 3)
-        dist(3, 2)
-        maxscan(2)
         ts(C("m1"), C("SM", 256, 512), C("colr1"), OP.is_equal)
-        cp(C("sl"), C("SM", 48, 64))
         tt(C("pm"), IND(C("pw", 0, 1024), C("us16")), C("m1"), OP.mult)
-        mms([(C("KN", 0, 256), C("bo256"), C("pm"), True, False)] + bcast("KN", 0, [C("f2b")], False) + [(C("KN", 0, 256), PB(0), C("lanep"), False, True)])
-        cp(U("wi", 2), C("kx", 527, 768, 16))
-        ts(U("wj", 2), U("wi", 2), 31, OP.bitwise_and)
-        cp(U("wb16", 2), U("wj", 2))
+        mms([(C("KN", 0, 256), C("bo256"), C("pm"), False, True)])
+        cp(U("wb16", 2), U("em", 3))
         vabs(3, 0)
         dist(3, 0)
         sabs(3, 3)
-        vget(3, 1, X3)
+        a3, n3 = LANES[1]
+        vpart(3, a3, PART, X3)
         mms(bcast("WB1", 0, [U("wb16", 2)], True))
-        dist(3, 3)
-        vabs(3, 1)
-        dist(3, 1)
-        tt(C("bm"), C("KN", 0, 256), C("mask"), OP.mult)
-        act(C("kb"), C("KN", 0, 256))
-        mms([(C("KN", 256, 512), C("bo32"), C("pm"), True, False)])
-        scan(C("bs"), C("sd0"), C("bm"), OP.mult, OP.add)
-        act(C("na"), C("bs", 15, 256, 16), AF.Copy, 0.5, -1.0)
-        ts(C("hm"), U("fc", 3), -1.0, OP.mult, 1.0, OP.add)
-        worst2(2, 1, "WB1")
-        tt(C("be"), C("em"), U("bp", 0, 3), OP.add)
-        ts(C("fin"), C("sl"), 64.0, OP.is_lt)
+        sdist(3)
+        vabs(3, 1, 0, PART // 16)
+        dist(3, 1, 0, PART // 16)
+        tt(C("be"), U("em", 0, 3), U("bp", 0, 3), OP.add)
+        ts(C("fin"), C("SM", 48, 64), 64.0, OP.is_lt)
         tt(C("hb"), C("hit"), C("be"), OP.mult)
         tt(C("fin"), C("fin"), U("fc", 3), OP.mult)
-        tt(C("ix"), U("hb", 0), U("hb", 1), OP.add)
-        ts(C("gp"), C("sl"), 3904.0 + 64 * t, OP.add)
-        tt(C("ix"), C("ix"), U("hb", 2), OP.add)
         tt(C("fud"), U("fc", 1, 3), C("ud"), OP.mult)
-        tt(C("ix"), C("ix"), C("dn"), OP.add)
-        tt(C("gp"), C("gp"), C("dx"), OP.subtract)
-        act(C("dd", 16384, 16384 + VL), C(q, 0, VL), AF.Copy, None, -1.0)
-        act(C("q2", 0, VL), C(q, 0, VL), AF.Copy, None, 2.0)
-        act(C("q2", VL, 256), C(q, VL, 256))
+        tt(C("bm"), C("KN", 0, 256), C("mask"), OP.mult)
+        act(C("kb"), C("KN", 0, 256))
+        act(C("WB1", 256, 512), C("WB1", 0, 256), AF.Square, C("colb"), 64.0)
+        mms([(C("KN", 256, 512), C("bo32"), C("pm"), True, False)])
+        scan(C("bs"), C("sd0"), C("bm"), OP.mult, OP.add)
+        ts(C("na"), C("bs", 15, 256, 16), -1.0, OP.mult, 0.5, OP.add)
         tt(C("nb"), C("na"), C("lu"), OP.add)
-        ts(C("nd"), C("nb"), 0.5, OP.subtract, -1.0 / 256, OP.mult)
-        tt(C("nd"), C("nd"), C("dx"), OP.subtract)
+        act(C("nd"), C("nb"), AF.Copy, 1.0 / 512, -1.0 / 256)
+        vpart(3, a3 + PART, n3 - PART, X3)
 
         def lowest(c0, c1):
             for c in range(c0, c1):
                 for k, o in (("na", "aa"), ("nb", "ab")):
                     act(C("junk", 0, 16 * c + 16), C("kb", 0, 16 * c + 16), AF.Sign, C(k, c, c + 1), None, C(o, c, c + 1))
 
-        lowest(0, split)
+        lowest(0, SPLIT0)
+        vabs(3, 1, PART // 16)
+        dist(3, 1, PART // 16)
+        ts(C("wm", 512, 768), C("WB1", 0, 256), C("cole"), OP.is_equal)
+        tt(C("lim", 512, 768), C("li32", 512, 768), C("WB1", 256, 512), OP.min)
+        mms([(C("SM", 64, 80), C("idm32"), x, i == 0, i == 3) for i, x in enumerate([U("hb", 0), U("hb", 1), U("hb", 2), C("dn")])])
+        act(C("dd", 16384, 16384 + VL), C(q, 0, VL), AF.Copy, None, -1.0)
+        act(C("q2", 0, VL), C(q, 0, VL), AF.Copy, None, 2.0)
+        act(C("q2", VL, 256), C(q, VL, 256))
+        mms([(C("WB0", 0, 256), C("idm"), C(q), True, True)])
+        tt(C("nd"), C("nd"), C("dx"), OP.subtract)
+        tt(C("nd"), C("nd"), C("hm"), OP.mult)
+        lowest(SPLIT0, split)
         minscan(3)
-        ts(C("c3"), C("km", 783, 1024, 16), C("tb32"), OP.is_lt)
-        cp(C("k3"), C("km", 783, 1024, 16))
+        ts(C("c3"), C("km", 1551, 1792, 16), C("tb32"), OP.is_lt)
+        cp(C("k3"), C("km", 1551, 1792, 16))
         tt(C("came"), C("c3"), C("fin"), OP.mult)
         ts(C("e3"), C("k3"), 31, OP.bitwise_and)
         tt(C("got"), C("came"), C("hm"), OP.add)
         tt(C("t3"), C("e3"), U("bp", 3), OP.add)
-        tt(C("cs"), C("came"), C("sl"), OP.mult)
+        tt(C("cs"), C("came"), C("SM", 48, 64), OP.mult)
         tt(C("i3"), C("t3"), C("came"), OP.mult)
         act(C("cc"), C("came"), AF.Copy, None, 3904.0 + 64 * t)
         for s in range(3):
             act(U("g48", s), C("got"))
         mms(bcast("KN", 256, [C("cs"), C("cc")], False) + [(C("KN", 256, 512), PB(0), C("zz"), False, True)])
-        tt(C("i3"), C("i3"), C("ix"), OP.add)
+        tt(C("i3"), C("i3"), C("SM", 64, 80), OP.add)
         cp(C("i316"), C("i3"))
-        tt(C("cg"), C("came"), C("gp"), OP.mult)
+        tt(C("cg"), C("came"), C("SM", 80, 96), OP.mult)
         tt(C("vi"), IND(C("dd"), C("i316")), C("q2"), OP.add)
         tt(C("og"), C("cg"), C("dx"), OP.add)
         if not last:
@@ -540,9 +555,10 @@ def rank_program(g, core, T, topo):
         if not last:
             cp(C(qn), C("vq"))
             starts(t + 1, qn)
+            spread(qn, "G")
             spread(qn, "S")
         lowest(split, 16)
-        tt(C("gv"), C("vi"), C(q), OP.subtract)
+        tt(C("gv"), C("vi"), C("WB0", 0, 256), OP.subtract)
         ts(C("hv"), C("vi"), 1, OP.arith_shift_right)
         cp(IND(C("xw"), C("og16")), C("gv"))
 
@@ -554,26 +570,27 @@ def rank_program(g, core, T, topo):
                     tt(C("so"), C("so"), C("dp"), OP.add)
                 if s == 1:
                     cp(C("so16"), C("so"))
+
+        def lists_in():
             for s in (2, 1, 0):
                 a, b = 256 * s, 256 * s + 256
                 tt(IND(C("pw"), U("so16", s)), C("lim", a, b), C("mn", a, b), OP.add)
 
         def records():
-            tt(C("df"), C("ab"), C("aa"), OP.subtract)
-            ts(C("okd"), C("df"), 1.0, OP.is_lt)
-            tt(C("okd"), C("okd"), C("hm"), OP.mult)
+            tt(C("okd"), C("ab"), C("aa"), OP.is_equal)
             tt(C("oh"), C("okd"), C("nd"), OP.mult)
             tt(C("oh"), C("oh"), C("dx"), OP.add)
             cp(C("oh16"), C("oh"))
             cp(IND(C("xw"), C("oh16")), C("hv"))
 
+        lists()
         if last:
             records()
             dma("oy", T.yx[:], T["xw"][:, 0:4096], [("xw", 0, 4096)], [])
-            lists()
+            lists_in()
             dma("op", T.yp[:], T["pw"][:, 0:1024], [("pw", 0, 1024)], [])
         else:
-            lists()
+            lists_in()
             start_towns()
             spread(qn, "V")
             records()

from concourse.mybir import AluOpType as OP, ActivationFunctionType as AF

R, N = 3, 4
BIG = 1000000.0
FAR = 2097152.0
LANES = [(0, 64), (64, 112), (176, 48), (224, 32)]
VL = 176
SPLIT0, SPLIT, PART = 4, 11, 64
POOL, VEC = (1, 5, 9, 13), (3, 11)
LEAST, MOST = [0, 256, 512, 1536], [1024, 1280, 768]

SCRATCH = {}
PLACE = {}
PS = ["K0", "K1", "SM", "WB0", "WB1", "KN", "SUB0", "SUB1"]


def _declare():
    f, b, i, u = "float32", "bfloat16", "int32", "uint16"
    sb = {}

    def add(d, text):
        for w in text.split():
            k, n = w.split(":")
            sb[k] = (int(n), d)

    add(b, "xw:4352 dd:16640 qr:4096 qf0:256 qf1:256 q2:256 mmb:16 f0h:16 f2h:16 f2b:16 te:48 junk:256 cum:24 wb16:48 got:16 gv:256 cs:16 cc:16")
    add(b, "bo:128 bw:144 bwf:144 pb:2048 rr:128 tri:128 sw:128 swi:128 idm:128 nid:128 dlt:16 lub:16 gcs:48 ep:256 zz:256 lanep:256")
    add(f, "pw:1288 mw:1024 th32:1 tb32:1 km:1792 bm:256 bs:256 b1:256 li32:768 lim:768 wm:768 mn:768 uu:48 fc:64 nft:32 hit:48 tu:48 us:16")
    add(f, "be:48 hb:48 hm:16 m1:256 pm:256 kb:256 na:16 nb:16 nd:16 aa:16 ab:16 okd:16 fin:16 ud:48 fud:48 g48:48 so:48")
    add(f, "ex:16 exd:16 xo:16 c3:16 came:16 t3:16 i3:16 oh:16 og:16 cg:16")
    add(f, "colr:1 colp:1 colg:1 colg15:1 colr1:1 cole:1 colb:1 par:1 colsw:1 cold:1 colp16:1 mr:256 mf:256 mg:256 mask:256 bo32:128 bo256:128 idm32:128")
    add(f, "mn0:256 mx0:256 sd0:256 one:16 lu:16 dp:48 dx:16 dn:16 bp:64")
    add(i, "twi:1024 thi:1 u0i:16 mmi:16 ki:64 em:64 wi:48 wj:48 k3:16 e3:16 vi:256 vq:256 hv:256 ip:1 il:16 pr:1 pp:1 b4:16")
    add(u, "us16:16 so16:48 xo16:16 i316:16 oh16:16 og16:16 li0:256 li1:256 li2:256 li3:256 uo0:16 uo1:16 uo2:16 uo3:16")
    for t in range(R):
        add(b, "xb%d:4096" % t)
        add(f, "pb%d:1032" % t)
    size = {}
    for k, (n, d) in sb.items():
        if n > 256 or k in ("qf0", "thi"):
            SCRATCH[k] = ("sbuf", [128, n], d)
            PLACE[k] = (k, 0, n)
        else:
            PLACE[k] = ("all_" + d, size.get(d, 0), n)
            size[d] = size.get(d, 0) + (n + 15) // 16 * 16
    for d in size:
        SCRATCH["all_" + d] = ("sbuf", [128, size[d]], d)
    for k in range(3):
        SCRATCH["ring%d" % k] = ("sbuf", [128, (LANES[k][1] if k < 2 else 256 - VL) // 16, 16, 16], b)
    SCRATCH["mo8"] = ("sbuf", [8, 1024], i)
    SCRATCH["mo8f"] = ("sbuf", [8, 1024], f)
    SCRATCH["sel8"] = ("sbuf", [8, 128], f)
    for k in PS:
        SCRATCH[k] = ("psum", [128, 512], f)
        PLACE[k] = (k, 0, 512)


_declare()
SEMAPHORES = ["sv", "sa", "st", "sg", "dq", "dx", "dt", "dh", "dm", "oy", "op", "om"] + ["%s%d" % (k, t) for k in ("ax", "ap", "lx", "lp") for t in range(R)]


def rank_program(g, core, T, topo):
    rank = T.rank_of(core)
    if rank is None:
        return
    ENG = {"V": g.vector, "S": g.scalar, "P": g.tensor, "G": g, "Y": g.sync}
    SEM = {"V": "sv", "S": "sa", "P": "st", "G": "sg"}
    count, known, hist = {}, {q: {} for q in ENG}, {}

    def wait_toks(q, toks):
        need = {}
        for (s, v, vc) in toks:
            if known[q].get(s, 0) < v and need.get(s, (0, None))[0] < v:
                need[s] = (v, vc)
        for s in list(need):
            if any(o != s and need[o][1].get(s, 0) >= need[s][0] for o in need):
                del need[s]
        for s in need:
            ENG[q].wait_ge(T.sem[s], need[s][0])
        for (s, v, vc) in toks:
            for k in vc:
                if known[q].get(k, 0) < vc[k]:
                    known[q][k] = vc[k]

    def deps(q, reads, writes):
        out = []
        for wr, regs in ((False, reads), (True, writes)):
            for (b, lo, hi) in regs:
                for (l, h, w, eq, tok) in hist.get(b, []):
                    same = eq == q
                    if b in PS and not same:
                        out.append(tok)
                    elif l < hi and lo < h and (w or wr):
                        if same and (q == "P" or not w):
                            continue
                        out.append(tok)
        return out

    def note(eq, reads, writes, tok):
        for (b, lo, hi) in writes:
            hist[b] = [e for e in hist.get(b, []) if not (lo <= e[0] and e[1] <= hi)] + [(lo, hi, True, eq, tok)]
        for (b, lo, hi) in reads:
            hist[b] = [e for e in hist.get(b, []) if not (not e[2] and e[3] == eq and eq in SEM and lo <= e[0] and e[1] <= hi)] + [(lo, hi, False, eq, tok)]

    def finish(q, sem, n, ins, reads, writes, eq):
        count[sem] = count.get(sem, 0) + n
        ins.then_inc(T.sem[sem], n)
        vc = dict(known[q])
        vc[sem] = count[sem]
        note(eq, reads, writes, (sem, count[sem], vc))

    def op(q, reads, writes, fn):
        wait_toks(q, deps(q, reads, writes))
        finish(q, SEM[q], 1, fn(), reads, writes, q)

    def dma(sem, out, in_, reads, writes):
        wait_toks("Y", deps("Y", reads, writes))
        finish("Y", sem, 16, g.sync.dma_start(out, in_), reads, writes, "dma")

    def C(name, a=0, b=None, st=1):
        buf, at, n = PLACE[name]
        b = n if b is None else b
        if name == "qr":
            return (T[buf][:, a:b:st], [("qr", a, a + 1)], []) if st == 16 else (T[buf][:, a:b], [("qr", 0, 16)], [])
        return (T[buf][:, at + a:at + b:st] if st != 1 else T[buf][:, at + a:at + b], [(name, a, b)], [])

    def U(name, s, n=1):
        return C(name, 16 * s, 16 * s + 16 * n)

    def PB(r):
        return C("pb", 128 * r, 128 * r + 128)

    def IND(w, o):
        return (w[0].indirect(o[0]), w[1], o[1])

    def rg(*xs):
        return [r for x in xs if isinstance(x, tuple) for r in x[1] + x[2]]

    def ap(x):
        return x[0] if isinstance(x, tuple) else x

    def tt(out, a, b, o):
        op("V", rg(a, b) + out[2], out[1], lambda: g.vector.tensor_tensor(out[0], a[0], b[0], o))

    def ts(out, a, s1, o1, s2=None, o2=None):
        if o2 is None:
            op("V", rg(a, s1), out[1], lambda: g.vector.tensor_scalar(out[0], a[0], ap(s1), None, o1))
        else:
            op("V", rg(a, s1, s2), out[1], lambda: g.vector.tensor_scalar(out[0], a[0], ap(s1), ap(s2), o1, o2))

    def cp(out, a):
        op("V", rg(a) + out[2], out[1], lambda: g.vector.tensor_copy(out[0], a[0]))

    def fill(out, k):
        op("V", [], out[1], lambda: g.vector.memset(out[0], k))

    def scan(out, d0, d1, o0, o1):
        op("V", rg(d0, d1), out[1], lambda: g.vector.tensor_tensor_scan(out[0], d0[0], d1[0], 0.0, o0, o1))

    def act(out, a, func=AF.Copy, bias=None, scale=None, acc=None):
        kw = {}
        if bias is not None:
            kw["bias"] = ap(bias)
        if scale is not None:
            kw["scale"] = ap(scale)
        if acc is not None:
            kw["accum_out"] = acc[0]
        op("S", rg(a, bias, scale), out[1] + (acc[1] if acc is not None else []), lambda: g.scalar.activation(out[0], a[0], func, **kw))

    def iota(x, pattern, start, by):
        op("G", [], x[1], lambda: g.iota(x[0], pattern, start, by, allow_small_or_imprecise_dtypes=True))

    def mms(lst):
        def go():
            for (o, l, r, a, b) in lst:
                ins = g.tensor.matmul(o[0], l[0], r[0], a, b)
            return ins
        op("P", [x for m in lst for x in m[1][1] + m[2][1]], [x for m in lst for x in m[0][1]], go)

    dma("dq", T["qf0"][:], T.qs[:], [], [("qf0", 0, 256)])
    dma("dt", T["twi"][:], T.towns[:], [], [("twi", 0, 1024)])
    dma("dx", T["xw"][:, 0:3904], T.x[:], [], [("xw", 0, 3904)])
    dma("dh", T["thi"][:], T.th[:], [], [("thi", 0, 1)])
    dma("dm", T["mo8"][:], T.mo[:], [], [("mo8", 0, 1024)])

    iota(C("ip"), [[0, 1]], 0, 1)
    iota(C("il"), [[16, 16]], 0, 1)
    iota(C("mf"), [[1, 256]], 0, 0)
    iota(C("mr"), [[0, 16], [1, 16]], 0, 0)
    iota(C("mg"), [[16, 16], [0, 16]], 0, 0)
    iota(C("ep"), [[0, 16], [1, 16]], 1, 0)
    iota(C("lanep"), [[1, 256]], 0, 0)
    ts(C("pr"), C("ip"), 15, OP.bitwise_and)
    cp(C("colp"), C("ip"))
    cp(C("colr"), C("pr"))
    tt(C("colg"), C("colp"), C("colr"), OP.subtract)
    ts(C("colr1"), C("colr"), 1.0, OP.add)
    ts(C("colg15"), C("colg"), 15.0, OP.add)
    ts(C("bwf"), C("mf", 0, 144), C("colg15"), OP.is_equal, C("colr1"), OP.mult)
    ts(C("lu"), C("il"), C("colg"), OP.subtract)
    ts(C("b4"), C("lu"), 4.0, OP.mult)
    ts(C("bo"), C("mg", 0, 128), C("colg"), OP.is_equal)
    ts(C("mask"), C("mr"), C("colr"), OP.is_equal)
    ts(C("bw"), C("mf", 0, 144), C("colg15"), OP.is_equal, 32.0, OP.mult)
    ts(C("idm"), C("mf", 0, 128), C("colp"), OP.is_equal)

    def spread(qn, where):
        for e in range(16):
            o = C("qr", e, 4096, 16)
            if e in POOL:
                if where == "G":
                    op("G", [(qn, 0, 256)], o[1], lambda: g.affine_select(o[0], C(qn)[0], [[0, 256]], OP.is_ge, 0.0, 0, 0))
            elif e in VEC:
                if where == "V":
                    cp(o, C(qn))
            elif where == "S":
                act(o, C(qn))

    def starts(t, qn):
        lst = [(C("SM", 0, 16), C("bwf", 15 - r, 143 - r), C(qn, r, 256, 16), r == 0, t == 0 and r == 15) for r in range(16)]
        if t:
            lst.append((C("SM", 0, 16), C("rr"), C("got"), False, True))
        mms(lst)

    def start_towns():
        cp(C("u0i"), C("SM", 0, 16))
        ts(C("mmi"), C("u0i"), 3, OP.bitwise_and)
        tt(U("uu", 0), C("mmi"), C("b4"), OP.add)
        cp(C("uo0"), U("uu", 0))

    def entries(s, P):
        cp(C("li%d" % s), IND(C(P, 0, 1024), C("uo%d" % s)))

    starts(0, "qf0")
    for e in range(16):
        act(C("qr", e, 4096, 16), C("qf0"))
    act(C("nid"), C("idm"), AF.Copy, None, -1.0)
    cp(C("pw", 0, 1024), C("twi"))
    start_towns()
    entries(0, "pw")
    fill(C("xw", 3904, 4096), 0.0)
    fill(C("pw", 1024, 1032), 0.0)
    cp(C("pw", 1024, 1025), C("thi"))

    def constants():
        for r in range(16):
            if r % 2:
                act(PB(r), C("bo"), AF.Identity, None, C("mask", r, r + 1))
            else:
                ts(PB(r), C("bo"), C("mask", r, r + 1), OP.mult)
        ts(C("th32"), C("thi"), 32.0, OP.mult)
        ts(C("mn0"), C("mr"), 0.0, OP.is_equal, 2.0 * BIG, OP.mult)
        ts(C("mn0"), C("mn0"), -BIG, OP.add)
        ts(C("sd0"), C("mr"), 0.0, OP.not_equal)
        ts(C("mx0"), C("mr"), 0.0, OP.is_equal, -BIG, OP.mult)
        ts(C("mx0"), C("mx0"), 2.0, OP.add)
        fill(C("dd", 16384 + VL, 16640), 0.0)

    def late_constants():
        ts(C("pp"), C("ip"), 1, OP.bitwise_and)
        cp(C("par"), C("pp"))
        ts(C("cole"), C("colr"), -1.0, OP.mult, 31.0, OP.add)
        ts(C("colb"), C("colr"), 64.0, OP.mult, -1984.0, OP.add)
        ts(C("colsw"), C("par"), -2.0, OP.mult, 1.0, OP.add)
        ts(C("cold"), C("par"), -8.0, OP.mult, 4.0, OP.add)
        tt(C("colsw"), C("colsw"), C("colp"), OP.add)
        ts(C("tri"), C("mr", 0, 128), C("colr"), OP.is_gt)
        tt(C("tri"), C("tri"), C("bo"), OP.mult)
        ts(C("sw"), C("mf", 0, 128), C("colsw"), OP.is_equal)
        tt(C("swi"), C("sw"), C("idm"), OP.subtract)
        ts(C("dlt"), C("mr", 0, 16), 0.0, OP.mult, C("cold"), OP.add)
        act(C("rr"), C("mask", 0, 128))
        ts(C("bo32"), C("mg", 0, 128), C("colg"), OP.is_equal)
        act(C("idm32"), C("idm"))
        act(C("lub"), C("lu"))
        for s in range(R):
            act(U("gcs", s), C("lu"), AF.Copy, 64.0 * s - 192.0, 0.0)
        act(C("bo256"), C("bo32"), AF.Copy, None, 256.0)
        fill(C("one"), 1.0)
        fill(C("fc", 0, 16), 1.0)
        fill(C("cum"), 0.0)
        fill(C("zz"), 0.0)
        for s in range(3):
            act(U("dp", s), C("lu"), AF.Copy, 1032.0)
        act(C("dx"), C("lu"), AF.Copy, 4096.0)
        act(C("dn"), C("lu"), AF.Copy, 16384.0)
        for s in range(4):
            act(U("bp", s), C("lu"), AF.Copy, 4096.0 * s - 16385.0, 15.0)

    def load_mothers():
        cp((T["mo8f"][:, :], [("mo8f", 0, 1024)], []), (T["mo8"][:, :], [("mo8", 0, 1024)], []))
        ts(C("colp16"), C("colp"), 16.0, OP.mult)
        bm, am, _ = PLACE["mg"]
        bc, ac, _ = PLACE["colp16"]
        op("V", [("mg", 0, 128), ("colp16", 0, 1)], [("sel8", 0, 128)], lambda: g.vector.tensor_scalar(T["sel8"][:, :], T[bm][0:8, am:am + 128], T[bc][0:8, ac:ac + 1], None, OP.is_equal))
        for h, b in ((0, "WB0"), (1, "WB1")):
            mms([(C(b), (T["sel8"][:, :], [("sel8", 0, 128)], []), (T["mo8f"][:, 512 * h:512 * h + 512], [("mo8f", 0, 1024)], []), True, True)])

    def keep_mothers():
        for h, b in ((0, "WB0"), (1, "WB1")):
            act(C("mw", 512 * h, 512 * h + 512), C(b))

    def send(t):
        dst, frm = T.cores[(rank - 1 - t) % N], T.cores[(rank + 1 + t) % N]
        rid, pid, _ = topo.addr(dst)
        for kind, src, dest, n in (("p", "pw", "pb%d" % t, 1032), ("x", "xw", "xb%d" % t, 4096)):
            wait_toks("G", deps("G", [(src, 0, n)], []))
            asem, lsem = "a%s%d" % (kind, t), "l%s%d" % (kind, t)
            g.remote_dma(T[dest][:, 0:n], T[src][:, 0:n], T.sem[asem], T.sem[lsem], pid, rid, topo.mask(core, dst))
            count[lsem] = len(topo.engines(core, dst))
            vc = dict(known["G"])
            vc[lsem] = count[lsem]
            note("dma", [(src, 0, n)], [], (lsem, count[lsem], vc))
            count[asem] = len(topo.engines(frm, core))
            note("dma", [], [(dest, 0, n)], (asem, count[asem], {asem: count[asem]}))

    def mother(s):
        tt(C("bm"), IND(C("mw"), C("uo%d" % s)), C("mask"), OP.mult)
        scan(C("bs"), C("sd0"), C("bm"), OP.mult, OP.add)
        cp(C("uo%d" % (s + 1)), C("bs", 15, 256, 16))
        if s < 2:
            act(U("uu", s + 1), C("bs", 15, 256, 16))

    def dcols(s, k):
        a, n = LANES[k]
        return C("dd", 4096 * s + 16 * a, 4096 * s + 16 * (a + n))

    def half(k, h):
        c = LANES[k][1] // 16
        lo, hi = (0, (c + 1) // 2) if h == 0 else ((c + 1) // 2, c)
        o = LANES[2][1] // 16 if k == 3 else 0
        return (T["ring2"][:, o + lo:o + hi, :, :], [("ring2", 256 * (o + lo), 256 * (o + hi))], []), 256 * lo, 256 * hi

    def vpart(s, a, n, X):
        tt(C("dd", 4096 * s + 16 * a, 4096 * s + 16 * (a + n)), IND(C(X, 0, 4096), C("li%d" % s, a, a + n)), C("qr", 16 * a, 16 * (a + n)), OP.subtract)

    def vget(s, k, X):
        vpart(s, LANES[k][0], LANES[k][1], X)

    def sget(s, k, X):
        a, n = LANES[k]
        act(dcols(s, k), IND(C(X, 0, 4096), C("li%d" % s, a, a + n)))

    def ssub(s, k):
        for h in range(2):
            _, lo, hi = half(k, h)
            a = 16 * LANES[k][0]
            o = C("SUB%d" % h, 0, hi - lo)
            mms([(o, C("nid"), C("qr", a + lo, a + hi), True, False), (o, C("idm"), C("dd", 4096 * s + a + lo, 4096 * s + a + hi), False, True)])

    def vabs(s, k, c0=0, c1=None):
        c1 = LANES[k][1] // 16 if c1 is None else c1
        n, a = "ring%d" % k, 4096 * s + 16 * LANES[k][0]
        act((T[n][:, c0:c1, :, :], [(n, 256 * c0, 256 * c1)], []), C("dd", a + 256 * c0, a + 256 * c1), AF.Abs)

    def sabs(s, k):
        for h in range(2):
            r, lo, hi = half(k, h)
            act(r, C("SUB%d" % h, 0, hi - lo), AF.Abs)

    def dist(s, k, c0=0, c1=None):
        c1 = LANES[k][1] // 16 if c1 is None else c1
        a, n = LANES[k][0] + 16 * c0, 16 * (c1 - c0)
        o = C("K%d" % (s % 2), a, a + n)
        rn = "ring%d" % k
        mms([(o, PB(0), C("ep", 0, n), True, False)] + [(o, C("bw", 15 - r, 143 - r), (T[rn][:, c0:c1, r, :], [(rn, 256 * c0, 256 * c1)], []), False, r == 15) for r in range(16)])

    def sdist(s):
        dist(s, 2, 0, (256 - VL) // 16)

    def sA(s, X):
        if s:
            sget(s, 2, X)
            ssub(s, 2)
        vabs(s, 0)
        dist(s, 0)
        sget(s, 3, X)
        sabs(s, 2)
        ssub(s, 3)

    def sB(s):
        vabs(s, 1)
        dist(s, 1)
        sabs(s, 3)
        sdist(s)

    def minscan(s):
        scan(C("km", LEAST[s], LEAST[s] + 256), C("mn0"), C("K%d" % (s % 2), 0, 256), OP.max, OP.min)

    def maxscan(s):
        scan(C("km", MOST[s], MOST[s] + 256), C("mx0"), C("K%d" % (s % 2), 0, 256), OP.add, OP.max)

    def bcast(bank, at, srcs, whole):
        return [(C(bank, at + r, at + 256, 16), PB(r), src, whole and i == 0, whole and i == len(srcs) - 1) for r in range(16) for i, src in enumerate(srcs)]

    for t in range(R):
        last = t == R - 1
        split = 16 if last else SPLIT
        q, qn = "qf%d" % (t % 2), "qf%d" % ((t + 1) % 2)
        X3, P3 = "xb%d" % t, "pb%d" % t
        if t:
            entries(0, "pw")
        vget(0, 0, "xw")
        sget(0, 2, "xw")
        ssub(0, 2)
        if t == 0:
            constants()
            load_mothers()
        vget(0, 1, "xw")
        if t == 0:
            send(0)
        sA(0, "xw")
        if t == 0:
            keep_mothers()
            late_constants()
        mother(0)
        entries(1, "pw")
        vget(1, 0, "xw")
        sB(0)
        mother(1)
        entries(2, "pw")
        vget(1, 1, "xw")
        act(C("b1"), IND(C("mw"), C("uo0")))
        cp(C("mmb"), C("mmi"))
        mother(2)
        minscan(0)
        maxscan(0)
        sA(1, "xw")
        ts(U("fc", 1), C("km", 15, 256, 16), C("th32"), OP.is_ge)
        cp(C("f0h"), U("fc", 1))
        act(C("li32", 0, 256), IND(C("pw", 0, 1024), C("uo0")))
        sB(1)
        mms([(C("SM", 16, 32), C("sw"), C("f0h"), True, True), (C("SM", 32, 48), C("swi"), C("mmb"), True, False), (C("SM", 32, 48), C("idm"), C("dlt"), False, True)])
        vget(2, 0, "xw")
        vget(2, 1, "xw")
        act(C("li32", 256, 512), IND(C("pw", 0, 1024), C("uo1")))
        minscan(1)
        maxscan(1)
        sA(2, "xw")
        tt(C("ex"), U("fc", 1), C("SM", 16, 32), OP.mult)
        tt(C("exd"), C("ex"), C("SM", 32, 48), OP.mult)
        tt(C("xo"), C("exd"), U("uu", 0), OP.add)
        cp(C("xo16"), C("xo"))
        cp(IND(C("mw"), C("xo16")), C("b1"))
        if last:
            dma("om", T.ym[:], T["mw"][0:128:16, :], [("mw", 0, 1024)], [])
        act(C("li32", 512, 768), IND(C("pw", 0, 1024), C("uo2")))
        cp(U("wi", 0, 2), C("km", 1039, 1536, 16))
        ts(U("wj", 0, 2), U("wi", 0, 2), 31, OP.bitwise_and)
        cp(U("wb16", 0, 2), U("wj", 0, 2))
        mms(bcast("WB0", 0, [U("wb16", 0)], True) + bcast("WB0", 256, [U("wb16", 1)], True))
        sB(2)
        entries(3, P3)
        vget(3, 0, X3)
        tt(C("ud"), C("uu"), C("dp"), OP.subtract)
        ts(C("wm", 0, 512), C("WB0"), C("cole"), OP.is_equal)
        act(C("WB0"), C("WB0"), AF.Square, C("colb"), 64.0)
        tt(C("lim", 0, 512), C("li32", 0, 512), C("WB0"), OP.min)
        act(C("tb32"), C(P3, 1024, 1025), AF.Copy, None, 32.0)
        sget(3, 2, X3)
        ssub(3, 2)
        minscan(2)
        maxscan(2)
        ts(C("nft"), C("km", 271, 768, 16), C("th32"), OP.is_ge)
        cp(C("ki"), C("km", 15, 1024, 16))
        tt(U("fc", 2), U("fc", 1), U("nft", 0), OP.mult)
        ts(C("em"), C("ki"), 31, OP.bitwise_and)
        tt(U("fc", 3), U("fc", 2), U("nft", 1), OP.mult)
        tt(C("hit"), U("fc", 0, 3), U("fc", 1, 3), OP.subtract)
        scan(C("cum", 1, 17), C("one"), U("fc", 3), OP.mult, OP.add)
        tt(C("te"), C("hit"), U("em", 0, 3), OP.mult)
        tt(C("tu"), C("hit"), C("uu"), OP.mult)
        tt(U("te", 0), U("te", 0), U("te", 1), OP.add)
        tt(C("us"), U("tu", 0), U("tu", 1), OP.add)
        tt(U("te", 0), U("te", 0), U("te", 2), OP.add)
        tt(C("us"), C("us"), U("tu", 2), OP.add)
        mms(bcast("SM", 256, [U("te", 0)], True))
        cp(C("us16"), C("us"))
        cp(C("f2h"), U("fc", 3))
        mms([(C("SM", 48, 64), C("bo"), C("cum", 0, 16), True, False), (C("SM", 48, 64), C("tri"), C("f2h"), False, True)])
        mms([(C("SM", 80, 96), l, x, i == 0, i == 3) for i, (l, x) in enumerate([(C("bo"), C("cum", 0, 16)), (C("tri"), C("f2h")), (C("nid"), C("lub")), (C("idm"), U("gcs", t))])])
        sget(3, 3, X3)
        act(C("f2b"), U("fc", 3), AF.Copy, None, FAR)
        act(C("hm"), U("fc", 3), AF.Copy, 1.0, -1.0)
        mms([(C("KN", 0, 256), PB(0), C("lanep"), True, False)] + bcast("KN", 0, [C("f2b")], False))
        sabs(3, 2)
        ssub(3, 3)
        ts(C("m1"), C("SM", 256, 512), C("colr1"), OP.is_equal)
        tt(C("pm"), IND(C("pw", 0, 1024), C("us16")), C("m1"), OP.mult)
        mms([(C("KN", 0, 256), C("bo256"), C("pm"), False, True)])
        cp(U("wb16", 2), U("em", 3))
        vabs(3, 0)
        dist(3, 0)
        sabs(3, 3)
        a3, n3 = LANES[1]
        vpart(3, a3, PART, X3)
        mms(bcast("WB1", 0, [U("wb16", 2)], True))
        sdist(3)
        vabs(3, 1, 0, PART // 16)
        dist(3, 1, 0, PART // 16)
        tt(C("be"), U("em", 0, 3), U("bp", 0, 3), OP.add)
        ts(C("fin"), C("SM", 48, 64), 64.0, OP.is_lt)
        tt(C("hb"), C("hit"), C("be"), OP.mult)
        tt(C("fin"), C("fin"), U("fc", 3), OP.mult)
        tt(C("fud"), U("fc", 1, 3), C("ud"), OP.mult)
        tt(C("bm"), C("KN", 0, 256), C("mask"), OP.mult)
        act(C("kb"), C("KN", 0, 256))
        act(C("WB1", 256, 512), C("WB1", 0, 256), AF.Square, C("colb"), 64.0)
        mms([(C("KN", 256, 512), C("bo32"), C("pm"), True, False)])
        scan(C("bs"), C("sd0"), C("bm"), OP.mult, OP.add)
        ts(C("na"), C("bs", 15, 256, 16), -1.0, OP.mult, 0.5, OP.add)
        tt(C("nb"), C("na"), C("lu"), OP.add)
        act(C("nd"), C("nb"), AF.Copy, 1.0 / 512, -1.0 / 256)
        vpart(3, a3 + PART, n3 - PART, X3)

        def lowest(c0, c1):
            for c in range(c0, c1):
                for k, o in (("na", "aa"), ("nb", "ab")):
                    act(C("junk", 0, 16 * c + 16), C("kb", 0, 16 * c + 16), AF.Sign, C(k, c, c + 1), None, C(o, c, c + 1))

        lowest(0, SPLIT0)
        vabs(3, 1, PART // 16)
        dist(3, 1, PART // 16)
        ts(C("wm", 512, 768), C("WB1", 0, 256), C("cole"), OP.is_equal)
        tt(C("lim", 512, 768), C("li32", 512, 768), C("WB1", 256, 512), OP.min)
        mms([(C("SM", 64, 80), C("idm32"), x, i == 0, i == 3) for i, x in enumerate([U("hb", 0), U("hb", 1), U("hb", 2), C("dn")])])
        act(C("dd", 16384, 16384 + VL), C(q, 0, VL), AF.Copy, None, -1.0)
        act(C("q2", 0, VL), C(q, 0, VL), AF.Copy, None, 2.0)
        act(C("q2", VL, 256), C(q, VL, 256))
        mms([(C("WB0", 0, 256), C("idm"), C(q), True, True)])
        tt(C("nd"), C("nd"), C("dx"), OP.subtract)
        tt(C("nd"), C("nd"), C("hm"), OP.mult)
        lowest(SPLIT0, split)
        minscan(3)
        ts(C("c3"), C("km", 1551, 1792, 16), C("tb32"), OP.is_lt)
        cp(C("k3"), C("km", 1551, 1792, 16))
        tt(C("came"), C("c3"), C("fin"), OP.mult)
        ts(C("e3"), C("k3"), 31, OP.bitwise_and)
        tt(C("got"), C("came"), C("hm"), OP.add)
        tt(C("t3"), C("e3"), U("bp", 3), OP.add)
        tt(C("cs"), C("came"), C("SM", 48, 64), OP.mult)
        tt(C("i3"), C("t3"), C("came"), OP.mult)
        act(C("cc"), C("came"), AF.Copy, None, 3904.0 + 64 * t)
        for s in range(3):
            act(U("g48", s), C("got"))
        mms(bcast("KN", 256, [C("cs"), C("cc")], False) + [(C("KN", 256, 512), PB(0), C("zz"), False, True)])
        tt(C("i3"), C("i3"), C("SM", 64, 80), OP.add)
        cp(C("i316"), C("i3"))
        tt(C("cg"), C("came"), C("SM", 80, 96), OP.mult)
        tt(C("vi"), IND(C("dd"), C("i316")), C("q2"), OP.add)
        tt(C("og"), C("cg"), C("dx"), OP.add)
        if not last:
            ts(C("vq"), C("vi"), 255, OP.bitwise_and)
        cp(C("og16"), C("og"))
        if not last:
            cp(C(qn), C("vq"))
            starts(t + 1, qn)
            spread(qn, "G")
            spread(qn, "S")
        lowest(split, 16)
        tt(C("gv"), C("vi"), C("WB0", 0, 256), OP.subtract)
        ts(C("hv"), C("vi"), 1, OP.arith_shift_right)
        cp(IND(C("xw"), C("og16")), C("gv"))

        def lists():
            tt(C("so"), C("fud"), C("g48"), OP.mult)
            for s in (2, 1, 0):
                tt(C("mn", 256 * s, 256 * s + 256), C("KN", 256, 512), C("wm", 256 * s, 256 * s + 256), OP.mult)
                if s == 2:
                    tt(C("so"), C("so"), C("dp"), OP.add)
                if s == 1:
                    cp(C("so16"), C("so"))

        def lists_in():
            for s in (2, 1, 0):
                a, b = 256 * s, 256 * s + 256
                tt(IND(C("pw"), U("so16", s)), C("lim", a, b), C("mn", a, b), OP.add)

        def records():
            tt(C("okd"), C("ab"), C("aa"), OP.is_equal)
            tt(C("oh"), C("okd"), C("nd"), OP.mult)
            tt(C("oh"), C("oh"), C("dx"), OP.add)
            cp(C("oh16"), C("oh"))
            cp(IND(C("xw"), C("oh16")), C("hv"))

        lists()
        if last:
            records()
            dma("oy", T.yx[:], T["xw"][:, 0:4096], [("xw", 0, 4096)], [])
            lists_in()
            dma("op", T.yp[:], T["pw"][:, 0:1024], [("pw", 0, 1024)], [])
        else:
            lists_in()
            start_towns()
            spread(qn, "V")
            records()
            send(t + 1)

    for s in count:
        if known["G"].get(s, 0) < count[s]:
            g.wait_ge(T.sem[s], count[s])
